import numpy as np
import ml_dtypes


def mxq(x, axis, fmt="e4m3"):
    dtype, down = {"e4m3": (ml_dtypes.float8_e4m3fn, 7), "e5m2": (ml_dtypes.float8_e5m2, 14)}[fmt]
    v = np.moveaxis(np.asarray(x, np.float32).astype(ml_dtypes.bfloat16).astype(np.float64), axis, -1)
    blocks = v.reshape(v.shape[:-1] + (-1, 32))
    amax = np.abs(blocks).max(-1, keepdims=True)
    byte = np.maximum(np.where(amax > 0, np.frexp(amax)[1] - 1 + 127, 0) - down, 1)
    scale = np.exp2(byte - 127.0)
    codes = (blocks / scale).astype(np.float32).astype(dtype).astype(np.float64)
    return np.moveaxis((codes * scale).reshape(v.shape), -1, axis)


WIDE = False


def mx_kscale(k):
    if not WIDE:
        return np.ones(k)
    levels = np.array([10, -10, 5, -5, 0])
    if k % 512:
        return np.exp2(np.random.permutation(np.resize(levels, k // 32))).repeat(32)
    a = np.empty((k // 512, 16))
    for p in range(k // 512):
        a[p, :8] = np.random.permutation(np.resize(levels, 8))
        for g in range(8):
            far = levels[np.abs(levels - a[p, g]) >= 10]
            a[p, g + 8] = far[np.random.randint(len(far))]
    return np.exp2(a.ravel()).repeat(32)


def f64(x):
    return np.asarray(x).astype(np.float64)


def striped(idx):
    return np.tile(idx.reshape(-1, 16).T, (8, 1)).astype(np.uint16)


def unstriped(offs):
    return offs[:16].T.reshape(-1).astype(np.int64)


E2M1 = np.array([0.0, 0.5, 1.0, 1.5, 2.0, 3.0, 4.0, 6.0, -0.0, -0.5, -1.0, -1.5, -2.0, -3.0, -4.0, -6.0])


def pack_weight(w, fmt):
    k, n = w.shape
    w = f64(np.asarray(w, np.float32).astype(ml_dtypes.bfloat16)).reshape(k // 32, 32, n)
    amax = np.abs(w).max(1)
    if fmt == "e4m3":
        byte = np.frexp(amax)[1] - 1 + 127 - 7
    else:
        mant, ex = np.frexp(amax / 6.0)
        byte = np.where(mant > 0.5, ex, ex - 1) + 127
    byte = np.clip(np.where(amax > 0, byte, 1), 1, 254)
    scaled = (w * np.exp2(127.0 - byte)[:, None, :]).reshape(k, n).astype(np.float32)
    by_word = np.ascontiguousarray(scaled.reshape(k // 512, 128, 4, n).transpose(0, 1, 3, 2))
    if fmt == "e4m3":
        words = by_word.astype(ml_dtypes.float8_e4m3fn).view(np.uint8)
    else:
        c = by_word.astype(ml_dtypes.float4_e2m1fn).view(np.uint8) & 0xF
        words = (c[..., 0::2] | (c[..., 1::2] << 4)).reshape(k // 512, 128, 2 * n)
    return np.ascontiguousarray(words), np.ascontiguousarray(byte.astype(np.uint8).reshape(k // 512, 16, n))


def unpack_weight(words, scales, fmt):
    g, _, n = scales.shape
    words = np.ascontiguousarray(words).reshape(g, 128, n, -1)
    if fmt == "e4m3":
        vals = words.view(ml_dtypes.float8_e4m3fn).astype(np.float64)
    else:
        nib = np.empty((g, 128, n, 4), np.uint8)
        nib[..., 0::2] = words & 0xF
        nib[..., 1::2] = words >> 4
        vals = E2M1[nib]
    vals = vals * np.repeat(np.exp2(scales.astype(np.float64) - 127.0), 8, axis=1)[..., None]
    return vals.transpose(0, 1, 3, 2).reshape(g * 512, n)


def gelu(v):
    return 0.5 * v * (1.0 + np.tanh(np.sqrt(2.0 / np.pi) * (v + 0.044715 * v**3)))


def often(T, S):
    return np.random.permutation(T)[(T * np.random.uniform(0, 1, S) ** 4).astype(np.int64)]


def bf(x):
    return np.asarray(x, np.float32).astype(ml_dtypes.bfloat16)


def planes(Y):
    n, m = Y.shape
    b = f64(bf(Y)).reshape(n // 32, 32, m)
    amax = np.abs(b).max(1)
    byte = np.clip(np.where(amax > 0, np.frexp(amax)[1] - 1 + 127 - 7, 1), 1, 254)
    codes = (b * np.exp2(127.0 - byte)[:, None, :]).reshape(n, m).astype(np.float32).astype(ml_dtypes.float8_e4m3fn).view(np.uint8)
    words = codes.reshape(n // 512, 128, 4, m).transpose(0, 1, 3, 2)
    return np.ascontiguousarray(words), np.ascontiguousarray(byte.astype(np.uint8).reshape(n // 512, 16, m))


K, K2, H, N, T, T2, S, P = 1024, 512, 1024, 1024, 4096, 2048, 1024, 512

def setup_inputs():
    n = np.random.standard_normal
    s = mx_kscale(K)[:, None]
    s2 = mx_kscale(K2)[:, None]
    u = mx_kscale(H)[:, None]
    tab_words, tab_scales = pack_weight(n((K, T)) * s, "e4m3")
    tab2_words, tab2_scales = pack_weight(n((K2, T2)) * s2, "e4m3")
    w1_words, w1_scales = pack_weight(n((K, H)) / np.sqrt(K) / s, "e2m1")
    w2 = n((K2, H)) / np.sqrt(K2) / s2 * u.T
    w3_words, w3_scales = pack_weight(n((H, N)) / np.sqrt(H) / u * np.exp(0.8 * n(N)), "e4m3")
    return {
        "tab_words": tab_words, "tab_scales": tab_scales,
        "offs": striped(np.random.permutation(T)[:S]),
        "pos1": striped(often(S, P)),
        "tab2_words": tab2_words, "tab2_scales": tab2_scales,
        "offs2": striped(np.random.permutation(T2)[:P]),
        "w1_words": w1_words, "w1_scales": w1_scales,
        "bias": (0.5 * n(H)).astype(np.float32),
        "w2": w2.astype(np.float32),
        "w3_words": w3_words, "w3_scales": w3_scales,
    }

def reference(tab_words, tab_scales, offs, pos1, tab2_words, tab2_scales, offs2,
              w1_words, w1_scales, bias, w2, w3_words, w3_scales):
    v = unpack_weight(tab_words, tab_scales, "e4m3")[:, unstriped(offs)]
    v2 = unpack_weight(tab2_words, tab2_scales, "e4m3")[:, unstriped(offs2)]
    w1 = unpack_weight(w1_words, w1_scales, "e2m1")
    w3 = unpack_weight(w3_words, w3_scales, "e4m3")
    pre = (w1.T @ v) + f64(bias)[:, None]
    err = mxq(f64(w2), 0, "e4m3").T @ v2
    th = np.tanh(pre[:, unstriped(pos1)])
    h = err * (1.0 - np.square(th))
    y = w3.T @ mxq(h, 0, "e4m3")
    words, scales = planes(y)
    return y, words, scales

@@ -1,0 +1,248 @@
+from contextlib import ExitStack
+
+import concourse.mybir as mybir
+
+F32 = mybir.dt.float32
+BF16 = mybir.dt.bfloat16
+I32 = mybir.dt.int32
+U32 = mybir.dt.uint32
+U16 = mybir.dt.uint16
+U8 = mybir.dt.uint8
+FP8X4 = mybir.dt.float8_e4m3fn_x4
+FP4X4 = mybir.dt.float4_e2m1fn_x4
+ACT = mybir.ActivationFunctionType
+ALU = mybir.AluOpType
+
+P = 128
+K, K2, H, N, T, T2, S, M = 1024, 512, 1024, 1024, 4096, 2048, 1024, 512
+BANK = 512
+CHUNKS = (256, 128, 128)
+FLOPS = 2 * (K * H * S + K2 * H * M + H * N * M)
+
+
+def tile_list_lineage_fitness_gradients_kernel(
+    tc, tab_words, tab_scales, offs, pos1, tab2_words, tab2_scales, offs2,
+    w1_words, w1_scales, bias, w2, w3_words, w3_scales, out_0, out_1, out_2,
+):
+    nc = tc.nc
+    with ExitStack() as ctx:
+        keep = ctx.enter_context(tc.tile_pool(name="keep", bufs=1))
+        ring = ctx.enter_context(tc.tile_pool(name="ring", bufs=2))
+        acc = ctx.enter_context(tc.psum_pool(name="acc", bufs=8))
+
+        def held(shape, dtype, name, tag=None):
+            return keep.tile(shape, dtype, name=name, tag=tag or name, align_bytes=64)
+
+        offs_sb = keep.tile([P, S // 16], U16, name="offs_sb")
+        pos_sb = keep.tile([P, M // 16], U16, name="pos_sb")
+        offs2_sb = keep.tile([P, M // 16], U16, name="offs2_sb")
+        tab_sc = held([P, T], U8, "tab_sc")
+        v_sc1 = held([P, S], U8, "v_sc1")
+        w1_sc_raw = held([P, 2 * H], U8, "w1_sc_raw")
+        tab2_sc = held([P, T2], U8, "tab2_sc")
+        w3_sc_raw = held([P, N], U8, "w3_sc_raw")
+        for plane in (tab_sc, tab2_sc, w1_sc_raw, v_sc1, w3_sc_raw):
+            nc.vector.memset(plane[:].bitcast(I32), 0)
+        w1_raw = held([P, 2 * 2 * H], U8, "w1_raw")
+        tab_w = [held([P, T], U32, f"tab_w{a}") for a in range(2)]
+        tab2_w = held([P, T2], U32, "tab2_w")
+        w2_raw = [held([P, 4, 512], F32, f"w2_raw{b}") for b in range(2)]
+        w3_raw = held([P, 2 * N], I32, "w3_raw")
+        bias_sb = held([P, 2, 4], F32, "bias_sb")
+        w2_rows = w2.rearrange("(p j) r -> p j r", j=4)
+
+        def load_tab(a):
+            nc.sync.dma_start(tab_w[a][:].bitcast(I32), tab_words[a].rearrange("p n i -> p (n i)").bitcast(I32))
+
+        nc.sync.dma_start(offs_sb[:], offs)
+        nc.sync.dma_start(offs2_sb[:], offs2)
+        nc.sync.dma_start(
+            w1_raw[:].bitcast(I32).rearrange("p (a c) -> p a c", a=2),
+            w1_words.bitcast(I32).rearrange("a p c -> p a c"),
+        )
+        for q in range(4):
+            nc.sync.dma_start(tab_sc[32 * q : 32 * q + 8, :].bitcast(I32), tab_scales[:, 4 * q : 4 * q + 4, :].bitcast(I32))
+        load_tab(0)
+        for q in range(4):
+            nc.sync.dma_start(
+                w1_sc_raw[32 * q : 32 * q + 4, :].bitcast(I32).rearrange("r (a c) -> r a c", a=2),
+                w1_scales[:, 4 * q : 4 * q + 4, :].bitcast(I32).rearrange("a r c -> r a c"),
+            )
+        load_tab(1)
+        nc.sync.dma_start(bias_sb[:], bias.rearrange("(b p t) -> p b t", b=2, t=4))
+        nc.sync.dma_start(pos_sb[:], pos1)
+        nc.sync.dma_start(tab2_w[:].bitcast(I32), tab2_words[0].rearrange("p n i -> p (n i)").bitcast(I32))
+        for q in range(4):
+            nc.gpsimd.dma_start(tab2_sc[32 * q : 32 * q + 4, :].bitcast(I32), tab2_scales[0, 4 * q : 4 * q + 4, :].bitcast(I32))
+        nc.sync.dma_start(w2_raw[0][:], w2_rows[:, :, 0:512])
+        nc.sync.dma_start(w2_raw[1][:], w2_rows[:, :, 512:1024])
+        for q in range(4):
+            nc.sync.dma_start(w3_sc_raw[32 * q : 32 * q + 8, :].bitcast(I32), w3_scales[:, 4 * q : 4 * q + 4, :].bitcast(I32))
+        nc.sync.dma_start(
+            w3_raw[:].rearrange("p (a c) -> p a c", a=2),
+            w3_words.rearrange("a p n i -> a p (n i)").bitcast(I32).rearrange("a p c -> p a c"),
+        )
+
+        def deal(dst, src, run):
+            nc.vector.tensor_copy(
+                out=dst.rearrange("p (g t u i) -> p g u t i", t=4, u=P // run, i=run),
+                in_=src.rearrange("p (g u i t) -> p g u t i", t=4, u=P // run, i=run),
+            )
+
+        v_sc = held([P, S], U8, "v_sc")
+        nc.vector.tensor_copy(v_sc[:], tab_sc[:].indirect(offs_sb[:]))
+        w1_w = held([P, 2 * 2 * H], U8, "w1_w")
+        deal(w1_w[:].bitcast(U16), w1_raw[:].bitcast(U16), 8)
+        nc.gpsimd.dma_start(v_sc1[0:100, :].bitcast(I32), v_sc[4:104, :].bitcast(I32))
+        w1_sc = held([P, 2 * H], U8, "w1_sc")
+        deal(w1_sc[:], w1_sc_raw[:], 16)
+
+        v_w = [[held([P, BANK], U32, f"v_w{a}{c}") for c in range(2)] for a in range(2)]
+        for a in range(2):
+            for c in range(2):
+                nc.vector.tensor_copy(v_w[a][c][:], tab_w[a][:].indirect(offs_sb[:, 32 * c : 32 * (c + 1)]))
+        v2_sc = held([P, M], U8, "v2_sc", tag="tab_w0")
+        nc.vector.tensor_copy(v2_sc[:], tab2_sc[:].indirect(offs2_sb[:]))
+        v_planes = [v_sc, v_sc1]
+
+        th = [held([P, S], F32, f"th{s}") for s in range(8)]
+
+        def pre_pass(bank, s, c, a):
+            col = a * H + s * P
+            nc.tensor.matmul_mx(
+                out=bank[:],
+                lhsT=w1_w[:, 2 * col : 2 * (col + P)].bitcast(FP4X4),
+                lhsT_scale=w1_sc[:, col : col + P],
+                rhs=v_w[a][c][:].bitcast(FP8X4),
+                rhs_scale=v_planes[a][:, c * BANK : (c + 1) * BANK],
+                start=(a == 0),
+                stop=(a == 1),
+            )
+
+        order = [(0, 0), (1, 0), (0, 1), (1, 1)] + [(s, c) for s in range(2, 8) for c in range(2)]
+        banks = {}
+        for s, c in order[:8]:
+            banks[(s, c)] = acc.tile([P, BANK], F32, name="bank")
+            pre_pass(banks[(s, c)], s, c, 0)
+        for s, c in order:
+            if (s, c) not in banks:
+                banks[(s, c)] = acc.tile([P, BANK], F32, name="bank")
+                pre_pass(banks[(s, c)], s, c, 0)
+            pre_pass(banks[(s, c)], s, c, 1)
+            nc.scalar.activation(
+                th[s][:, c * BANK : (c + 1) * BANK], banks[(s, c)][:], ACT.Tanh,
+                bias=bias_sb[:, s // 4, s % 4 : s % 4 + 1],
+            )
+
+        starts = [sum(CHUNKS[:i]) for i in range(len(CHUNKS))]
+        picked = [held([P, 4, M], F32, f"picked{b}") for b in range(2)]
+
+        def pick(b):
+            for t in range(4):
+                nc.vector.tensor_copy(picked[b][:, t, :], th[4 * b + t][:].indirect(pos_sb[:]))
+
+        w2_w = [held([P, 512], U32, f"w2_w{b}") for b in range(2)]
+        w2_sc = [held([P, 512], U8, f"w2_sc{b}") for b in range(2)]
+
+        w2_both = held([P, 4096], BF16, "w2_both", tag="w1_w")
+
+        def quantise_w2(b):
+            w2_bf = w2_both[:, 2048 * b : 2048 * (b + 1)]
+            nc.scalar.activation(
+                w2_bf.rearrange("p (t m j) -> p m t j", t=4, j=4),
+                w2_raw[b][:].rearrange("p j (m t) -> p m t j", t=4),
+                ACT.Copy, scale=-1.0,
+            )
+            nc.vector.quantize_mx(out=w2_w[b][:].bitcast(FP8X4), scales=w2_sc[b][:], in_=w2_bf)
+
+        v2_w = held([P, M], U32, "v2_w")
+        h_w = {}
+        h_sc = {}
+
+        def make_h(i, b):
+            m0, mc = starts[i], CHUNKS[i]
+            sq = held([P, mc * 4], F32, f"sq{i}{b}", tag=("w1_sc" if b == 0 else "sq1"))
+            nc.scalar.activation(
+                sq[:].rearrange("p (m t) -> p m t", t=4),
+                picked[b][:, :, m0 : m0 + mc].rearrange("p t m -> p m t"),
+                ACT.Square,
+            )
+            h_bf = held([P, mc * 4], BF16, f"h_bf{i}{b}")
+            for u in range(mc // P):
+                err = acc.tile([P, 4, P], F32, name="bank")
+                cols = slice(m0 + u * P, m0 + (u + 1) * P)
+                for t in range(4):
+                    nc.tensor.matmul_mx(
+                        out=err[:, t, :],
+                        lhsT=w2_w[b][:, t * P : (t + 1) * P].bitcast(FP8X4),
+                        lhsT_scale=w2_sc[b][:, t * P : (t + 1) * P],
+                        rhs=v2_w[:, cols].bitcast(FP8X4),
+                        rhs_scale=v2_sc[:, cols],
+                        start=True,
+                        stop=True,
+                    )
+                nc.vector.scalar_tensor_tensor(
+                    out=h_bf[:, u * BANK : (u + 1) * BANK].rearrange("p (m t) -> p m t", t=4),
+                    in0=sq[:, u * BANK : (u + 1) * BANK].rearrange("p (m t) -> p m t", t=4),
+                    scalar=1.0,
+                    in1=err[:].rearrange("p t m -> p m t"),
+                    op0=ALU.subtract,
+                    op1=ALU.mult,
+                )
+            h_w[(i, b)] = held([P, mc], U32, f"h_w{i}{b}")
+            h_sc[(i, b)] = held([P, mc], U8, f"h_sc{i}{b}")
+            nc.vector.quantize_mx(out=h_w[(i, b)][:].bitcast(FP8X4), scales=h_sc[(i, b)][:], in_=h_bf[:])
+
+        w3_w = held([P, 2 * N], I32, "w3_w")
+        w3_sc = held([P, N], U8, "w3_sc")
+        y_sc = held([P, 2, M], U8, "y_sc")
+        y_rows = out_0.rearrange("(g p t) m -> g p t m", g=2, t=4)
+        y_words = out_1.rearrange("g p m i -> g p (m i)").bitcast(I32).rearrange("g p m -> p g m")
+
+        def make_y(i):
+            m0, mc = starts[i], CHUNKS[i]
+            per_bank = BANK // mc
+            y_w = held([P, 2, mc], U32, f"y_w{i}")
+            for g in range(2):
+                y_sb = held([P, 4, mc], F32, f"y_sb{i}{g}")
+                for t0 in range(0, 4, per_bank):
+                    bank = acc.tile([P, BANK], F32, name="bank")
+                    for t in range(t0, t0 + per_bank):
+                        col = (4 * g + t) * P
+                        for a in range(2):
+                            nc.tensor.matmul_mx(
+                                out=bank[:, (t - t0) * mc : (t - t0 + 1) * mc],
+                                lhsT=w3_w[:, a * N + col : a * N + col + P].bitcast(FP8X4),
+                                lhsT_scale=w3_sc[4 * a : P, col : col + P],
+                                rhs=h_w[(i, a)][:].bitcast(FP8X4),
+                                rhs_scale=h_sc[(i, a)][:],
+                                start=(a == 0),
+                                stop=(a == 1),
+                            )
+                    nc.scalar.copy(y_sb[:, t0 : t0 + per_bank, :].rearrange("p t m -> p (t m)"), bank[:])
+                nc.sync.dma_start(y_rows[g][:, :, m0 : m0 + mc], y_sb[:])
+                y_bf = ring.tile([P, mc * 4], BF16, name=f"y_bf{i}", align_bytes=64)
+                nc.vector.tensor_copy(
+                    out=y_bf[:].rearrange("p (c i t) -> p c t i", i=4, t=4),
+                    in_=y_sb[:].rearrange("p t (c i) -> p c t i", i=4),
+                )
+                nc.vector.quantize_mx(out=y_w[:, g, :].bitcast(FP8X4), scales=y_sc[:, g, m0 : m0 + mc], in_=y_bf[:])
+            nc.sync.dma_start(y_words[:, :, m0 : m0 + mc], y_w[:].bitcast(I32))
+
+        nc.vector.tensor_copy(v2_w[:], tab2_w[:].indirect(offs2_sb[:]))
+        pick(0)
+        pick(1)
+        quantise_w2(0)
+        deal(w3_w[:], w3_raw[:], 4)
+        make_h(0, 0)
+        quantise_w2(1)
+        deal(w3_sc[:], w3_sc_raw[:], 16)
+        make_h(0, 1)
+        for i in range(1, len(CHUNKS)):
+            make_h(i, 0)
+            make_h(i, 1)
+            make_y(i - 1)
+        make_y(len(CHUNKS) - 1)
+        y_scale_rows = out_2.bitcast(I32).rearrange("g q m -> q g m")
+        for q in range(4):
+            nc.scalar.dma_start(y_scale_rows[4 * q : 4 * q + 4], y_sc[32 * q : 32 * q + 4].bitcast(I32))

@@ -16,7 +16,7 @@ ALU = mybir.AluOpType
 P = 128
 K, K2, H, N, T, T2, S, M = 1024, 512, 1024, 1024, 4096, 2048, 1024, 512
 BANK = 512
-CHUNKS = (256, 128, 128)
+CHUNKS = 4
 FLOPS = 2 * (K * H * S + K2 * H * M + H * N * M)
 
 
@@ -27,7 +27,6 @@ def tile_list_lineage_fitness_gradients_kernel(
     nc = tc.nc
     with ExitStack() as ctx:
         keep = ctx.enter_context(tc.tile_pool(name="keep", bufs=1))
-        ring = ctx.enter_context(tc.tile_pool(name="ring", bufs=2))
         acc = ctx.enter_context(tc.psum_pool(name="acc", bufs=8))
 
         def held(shape, dtype, name, tag=None):
@@ -41,14 +40,14 @@ def tile_list_lineage_fitness_gradients_kernel(
         w1_sc_raw = held([P, 2 * H], U8, "w1_sc_raw")
         tab2_sc = held([P, T2], U8, "tab2_sc")
         w3_sc_raw = held([P, N], U8, "w3_sc_raw")
-        for plane in (tab_sc, tab2_sc, w1_sc_raw, v_sc1, w3_sc_raw):
+        for plane in (tab_sc, w1_sc_raw, v_sc1, tab2_sc, w3_sc_raw):
             nc.vector.memset(plane[:].bitcast(I32), 0)
         w1_raw = held([P, 2 * 2 * H], U8, "w1_raw")
         tab_w = [held([P, T], U32, f"tab_w{a}") for a in range(2)]
+        bias_sb = held([P, 2, 4], F32, "bias_sb")
         tab2_w = held([P, T2], U32, "tab2_w")
         w2_raw = [held([P, 4, 512], F32, f"w2_raw{b}") for b in range(2)]
         w3_raw = held([P, 2 * N], I32, "w3_raw")
-        bias_sb = held([P, 2, 4], F32, "bias_sb")
         w2_rows = w2.rearrange("(p j) r -> p j r", j=4)
 
         def load_tab(a):
@@ -56,6 +55,7 @@ def tile_list_lineage_fitness_gradients_kernel(
 
         nc.sync.dma_start(offs_sb[:], offs)
         nc.sync.dma_start(offs2_sb[:], offs2)
+        nc.sync.dma_start(pos_sb[:], pos1)
         nc.sync.dma_start(
             w1_raw[:].bitcast(I32).rearrange("p (a c) -> p a c", a=2),
             w1_words.bitcast(I32).rearrange("a p c -> p a c"),
@@ -68,20 +68,19 @@ def tile_list_lineage_fitness_gradients_kernel(
                 w1_sc_raw[32 * q : 32 * q + 4, :].bitcast(I32).rearrange("r (a c) -> r a c", a=2),
                 w1_scales[:, 4 * q : 4 * q + 4, :].bitcast(I32).rearrange("a r c -> r a c"),
             )
-        load_tab(1)
         nc.sync.dma_start(bias_sb[:], bias.rearrange("(b p t) -> p b t", b=2, t=4))
-        nc.sync.dma_start(pos_sb[:], pos1)
+        load_tab(1)
         nc.sync.dma_start(tab2_w[:].bitcast(I32), tab2_words[0].rearrange("p n i -> p (n i)").bitcast(I32))
-        for q in range(4):
-            nc.gpsimd.dma_start(tab2_sc[32 * q : 32 * q + 4, :].bitcast(I32), tab2_scales[0, 4 * q : 4 * q + 4, :].bitcast(I32))
         nc.sync.dma_start(w2_raw[0][:], w2_rows[:, :, 0:512])
-        nc.sync.dma_start(w2_raw[1][:], w2_rows[:, :, 512:1024])
         for q in range(4):
-            nc.sync.dma_start(w3_sc_raw[32 * q : 32 * q + 8, :].bitcast(I32), w3_scales[:, 4 * q : 4 * q + 4, :].bitcast(I32))
+            nc.sync.dma_start(tab2_sc[32 * q : 32 * q + 4, :].bitcast(I32), tab2_scales[0, 4 * q : 4 * q + 4, :].bitcast(I32))
+        nc.sync.dma_start(w2_raw[1][:], w2_rows[:, :, 512:1024])
         nc.sync.dma_start(
             w3_raw[:].rearrange("p (a c) -> p a c", a=2),
             w3_words.rearrange("a p n i -> a p (n i)").bitcast(I32).rearrange("a p c -> p a c"),
         )
+        for q in range(4):
+            nc.sync.dma_start(w3_sc_raw[32 * q : 32 * q + 8, :].bitcast(I32), w3_scales[:, 4 * q : 4 * q + 4, :].bitcast(I32))
 
         def deal(dst, src, run):
             nc.vector.tensor_copy(
@@ -91,18 +90,20 @@ def tile_list_lineage_fitness_gradients_kernel(
 
         v_sc = held([P, S], U8, "v_sc")
         nc.vector.tensor_copy(v_sc[:], tab_sc[:].indirect(offs_sb[:]))
+        nc.scalar.dma_start(v_sc1[0:100, :].bitcast(I32), v_sc[4:104, :].bitcast(I32))
         w1_w = held([P, 2 * 2 * H], U8, "w1_w")
         deal(w1_w[:].bitcast(U16), w1_raw[:].bitcast(U16), 8)
-        nc.gpsimd.dma_start(v_sc1[0:100, :].bitcast(I32), v_sc[4:104, :].bitcast(I32))
         w1_sc = held([P, 2 * H], U8, "w1_sc")
-        deal(w1_sc[:], w1_sc_raw[:], 16)
-
         v_w = [[held([P, BANK], U32, f"v_w{a}{c}") for c in range(2)] for a in range(2)]
-        for a in range(2):
-            for c in range(2):
-                nc.vector.tensor_copy(v_w[a][c][:], tab_w[a][:].indirect(offs_sb[:, 32 * c : 32 * (c + 1)]))
-        v2_sc = held([P, M], U8, "v2_sc", tag="tab_w0")
-        nc.vector.tensor_copy(v2_sc[:], tab2_sc[:].indirect(offs2_sb[:]))
+
+        def look_up(a, c):
+            nc.vector.tensor_copy(v_w[a][c][:], tab_w[a][:].indirect(offs_sb[:, 32 * c : 32 * (c + 1)]))
+
+        for c in range(2):
+            look_up(0, c)
+            deal(w1_sc[:, c * H : (c + 1) * H], w1_sc_raw[:, c * H : (c + 1) * H], 16)
+        for c in range(2):
+            look_up(1, c)
         v_planes = [v_sc, v_sc1]
 
         th = [held([P, S], F32, f"th{s}") for s in range(8)]
@@ -121,7 +122,7 @@ def tile_list_lineage_fitness_gradients_kernel(
 
         order = [(0, 0), (1, 0), (0, 1), (1, 1)] + [(s, c) for s in range(2, 8) for c in range(2)]
         banks = {}
-        for s, c in order[:8]:
+        for s, c in sorted(order[:6], key=lambda sc: sc[1]):
             banks[(s, c)] = acc.tile([P, BANK], F32, name="bank")
             pre_pass(banks[(s, c)], s, c, 0)
         for s, c in order:
@@ -134,64 +135,72 @@ def tile_list_lineage_fitness_gradients_kernel(
                 bias=bias_sb[:, s // 4, s % 4 : s % 4 + 1],
             )
 
-        starts = [sum(CHUNKS[:i]) for i in range(len(CHUNKS))]
-        picked = [held([P, 4, M], F32, f"picked{b}") for b in range(2)]
+        picked = {}
 
-        def pick(b):
+        def pick(chunks, b, tag=None):
+            width = len(chunks) * P
+            tile = held([P, 4, width], F32, f"picked{chunks[0]}{b}", tag)
+            offsets = pos_sb[:, 8 * chunks[0] : 8 * (chunks[-1] + 1)]
             for t in range(4):
-                nc.vector.tensor_copy(picked[b][:, t, :], th[4 * b + t][:].indirect(pos_sb[:]))
+                nc.vector.tensor_copy(tile[:, t, :], th[4 * b + t][:].indirect(offsets))
+            for n, i in enumerate(chunks):
+                picked[(i, b)] = tile[:, :, n * P : (n + 1) * P]
 
         w2_w = [held([P, 512], U32, f"w2_w{b}") for b in range(2)]
         w2_sc = [held([P, 512], U8, f"w2_sc{b}") for b in range(2)]
 
-        w2_both = held([P, 4096], BF16, "w2_both", tag="w1_w")
+        w2_both = held([P, 4096], BF16, "w2_both")
 
         def quantise_w2(b):
             w2_bf = w2_both[:, 2048 * b : 2048 * (b + 1)]
-            nc.scalar.activation(
-                w2_bf.rearrange("p (t m j) -> p m t j", t=4, j=4),
-                w2_raw[b][:].rearrange("p j (m t) -> p m t j", t=4),
-                ACT.Copy, scale=-1.0,
+            nc.gpsimd.tensor_scalar(
+                out=w2_bf.rearrange("p (t m j) -> p m t j", t=4, j=4),
+                in0=w2_raw[b][:].rearrange("p j (m t) -> p m t j", t=4),
+                scalar1=-1.0,
+                scalar2=0.0,
+                op0=ALU.mult,
+                op1=ALU.add,
             )
             nc.vector.quantize_mx(out=w2_w[b][:].bitcast(FP8X4), scales=w2_sc[b][:], in_=w2_bf)
 
         v2_w = held([P, M], U32, "v2_w")
+        v2_sc = held([P, M], U8, "v2_sc")
         h_w = {}
         h_sc = {}
 
+        sq = {}
+
+        def square(i, b, tag=None):
+            sq[(i, b)] = held([P, P, 4], F32, f"sq{i}{b}", tag)
+            nc.scalar.activation(sq[(i, b)][:], picked[(i, b)].rearrange("p t m -> p m t"), ACT.Square)
+
         def make_h(i, b):
-            m0, mc = starts[i], CHUNKS[i]
-            sq = held([P, mc * 4], F32, f"sq{i}{b}", tag=("w1_sc" if b == 0 else "sq1"))
-            nc.scalar.activation(
-                sq[:].rearrange("p (m t) -> p m t", t=4),
-                picked[b][:, :, m0 : m0 + mc].rearrange("p t m -> p m t"),
-                ACT.Square,
-            )
-            h_bf = held([P, mc * 4], BF16, f"h_bf{i}{b}")
-            for u in range(mc // P):
-                err = acc.tile([P, 4, P], F32, name="bank")
-                cols = slice(m0 + u * P, m0 + (u + 1) * P)
-                for t in range(4):
-                    nc.tensor.matmul_mx(
-                        out=err[:, t, :],
-                        lhsT=w2_w[b][:, t * P : (t + 1) * P].bitcast(FP8X4),
-                        lhsT_scale=w2_sc[b][:, t * P : (t + 1) * P],
-                        rhs=v2_w[:, cols].bitcast(FP8X4),
-                        rhs_scale=v2_sc[:, cols],
-                        start=True,
-                        stop=True,
-                    )
-                nc.vector.scalar_tensor_tensor(
-                    out=h_bf[:, u * BANK : (u + 1) * BANK].rearrange("p (m t) -> p m t", t=4),
-                    in0=sq[:, u * BANK : (u + 1) * BANK].rearrange("p (m t) -> p m t", t=4),
-                    scalar=1.0,
-                    in1=err[:].rearrange("p t m -> p m t"),
-                    op0=ALU.subtract,
-                    op1=ALU.mult,
+            cols = slice(i * P, (i + 1) * P)
+            err = acc.tile([P, 4, P], F32, name="bank")
+            for t in range(4):
+                nc.tensor.matmul_mx(
+                    out=err[:, t, :],
+                    lhsT=w2_w[b][:, t * P : (t + 1) * P].bitcast(FP8X4),
+                    lhsT_scale=w2_sc[b][:, t * P : (t + 1) * P],
+                    rhs=v2_w[:, cols].bitcast(FP8X4),
+                    rhs_scale=v2_sc[:, cols],
+                    start=True,
+                    stop=True,
                 )
-            h_w[(i, b)] = held([P, mc], U32, f"h_w{i}{b}")
-            h_sc[(i, b)] = held([P, mc], U8, f"h_sc{i}{b}")
-            nc.vector.quantize_mx(out=h_w[(i, b)][:].bitcast(FP8X4), scales=h_sc[(i, b)][:], in_=h_bf[:])
+            h_bf = held([P, P, 4], BF16, f"h_bf{i}{b}")
+            nc.vector.scalar_tensor_tensor(
+                out=h_bf[:],
+                in0=sq[(i, b)][:],
+                scalar=1.0,
+                in1=err[:].rearrange("p t m -> p m t"),
+                op0=ALU.subtract,
+                op1=ALU.mult,
+            )
+            h_w[(i, b)] = held([P, P], U32, f"h_w{i}{b}")
+            h_sc[(i, b)] = held([P, P], U8, f"h_sc{i}{b}")
+            nc.vector.quantize_mx(
+                out=h_w[(i, b)][:].bitcast(FP8X4), scales=h_sc[(i, b)][:], in_=h_bf[:].rearrange("p m t -> p (m t)")
+            )
 
         w3_w = held([P, 2 * N], I32, "w3_w")
         w3_sc = held([P, N], U8, "w3_sc")
@@ -199,50 +208,65 @@ def tile_list_lineage_fitness_gradients_kernel(
         y_rows = out_0.rearrange("(g p t) m -> g p t m", g=2, t=4)
         y_words = out_1.rearrange("g p m i -> g p (m i)").bitcast(I32).rearrange("g p m -> p g m")
 
-        def make_y(i):
-            m0, mc = starts[i], CHUNKS[i]
-            per_bank = BANK // mc
-            y_w = held([P, 2, mc], U32, f"y_w{i}")
-            for g in range(2):
-                y_sb = held([P, 4, mc], F32, f"y_sb{i}{g}")
-                for t0 in range(0, 4, per_bank):
-                    bank = acc.tile([P, BANK], F32, name="bank")
-                    for t in range(t0, t0 + per_bank):
-                        col = (4 * g + t) * P
-                        for a in range(2):
-                            nc.tensor.matmul_mx(
-                                out=bank[:, (t - t0) * mc : (t - t0 + 1) * mc],
-                                lhsT=w3_w[:, a * N + col : a * N + col + P].bitcast(FP8X4),
-                                lhsT_scale=w3_sc[4 * a : P, col : col + P],
-                                rhs=h_w[(i, a)][:].bitcast(FP8X4),
-                                rhs_scale=h_sc[(i, a)][:],
-                                start=(a == 0),
-                                stop=(a == 1),
-                            )
-                    nc.scalar.copy(y_sb[:, t0 : t0 + per_bank, :].rearrange("p t m -> p (t m)"), bank[:])
-                nc.sync.dma_start(y_rows[g][:, :, m0 : m0 + mc], y_sb[:])
-                y_bf = ring.tile([P, mc * 4], BF16, name=f"y_bf{i}", align_bytes=64)
-                nc.vector.tensor_copy(
-                    out=y_bf[:].rearrange("p (c i t) -> p c t i", i=4, t=4),
-                    in_=y_sb[:].rearrange("p t (c i) -> p c t i", i=4),
-                )
-                nc.vector.quantize_mx(out=y_w[:, g, :].bitcast(FP8X4), scales=y_sc[:, g, m0 : m0 + mc], in_=y_bf[:])
-            nc.sync.dma_start(y_words[:, :, m0 : m0 + mc], y_w[:].bitcast(I32))
+        y_w = [held([P, 2, P], U32, f"y_w{i}") for i in range(CHUNKS)]
+
+        def make_y(i, g):
+            cols = slice(i * P, (i + 1) * P)
+            y_sb = held([P, 4, P], F32, f"y_sb{i}{g}")
+            y_bf = held([P, P, 4], BF16, f"y_bf{i}{g}")
+            bank = acc.tile([P, 4, P], F32, name="bank")
+            for t in range(4):
+                col = (4 * g + t) * P
+                for a in range(2):
+                    nc.tensor.matmul_mx(
+                        out=bank[:, t, :],
+                        lhsT=w3_w[:, a * N + col : a * N + col + P].bitcast(FP8X4),
+                        lhsT_scale=w3_sc[4 * a : P, col : col + P],
+                        rhs=h_w[(i, a)][:].bitcast(FP8X4),
+                        rhs_scale=h_sc[(i, a)][:],
+                        start=(a == 0),
+                        stop=(a == 1),
+                    )
+            if i == CHUNKS - 1:
+                nc.vector.tensor_copy(y_bf[:], bank[:].rearrange("p t m -> p m t"))
+                nc.scalar.copy(y_sb[:], bank[:])
+            else:
+                nc.scalar.copy(y_sb[:], bank[:])
+                nc.scalar.copy(y_bf[:], bank[:].rearrange("p t m -> p m t"))
+            nc.sync.dma_start(y_rows[g][:, :, cols], y_sb[:])
+            nc.vector.quantize_mx(
+                out=y_w[i][:, g, :].bitcast(FP8X4), scales=y_sc[:, g, cols], in_=y_bf[:].rearrange("p m t -> p (m t)")
+            )
+            if g == 1:
+                nc.sync.dma_start(y_words[:, :, cols], y_w[i][:].bitcast(I32))
 
         nc.vector.tensor_copy(v2_w[:], tab2_w[:].indirect(offs2_sb[:]))
-        pick(0)
-        pick(1)
+        pick((0, 1), 0)
+        nc.vector.tensor_copy(v2_sc[:], tab2_sc[:].indirect(offs2_sb[:]))
+        pick((0, 1), 1)
         quantise_w2(0)
-        deal(w3_w[:], w3_raw[:], 4)
-        make_h(0, 0)
         quantise_w2(1)
+        deal(w3_w[:], w3_raw[:], 4)
         deal(w3_sc[:], w3_sc_raw[:], 16)
+        square(0, 0, "w1_sc")
+        make_h(0, 0)
+        square(0, 1)
         make_h(0, 1)
-        for i in range(1, len(CHUNKS)):
-            make_h(i, 0)
-            make_h(i, 1)
-            make_y(i - 1)
-        make_y(len(CHUNKS) - 1)
+        square(1, 0, "w1_w")
+        square(1, 1)
+        make_h(1, 0)
+        make_h(1, 1)
+        for i in (2, 3):
+            pick((i,), 0, f"sq{i - 2}1")
+            pick((i,), 1, f"h_bf{i - 2}1")
+            for b in range(2):
+                make_y(i - 2, b)
+                square(i, b)
+            for b in range(2):
+                make_h(i, b)
+        for i in (2, 3):
+            for g in range(2):
+                make_y(i, g)
         y_scale_rows = out_2.bitcast(I32).rearrange("g q m -> q g m")
         for q in range(4):
-            nc.scalar.dma_start(y_scale_rows[4 * q : 4 * q + 4], y_sc[32 * q : 32 * q + 4].bitcast(I32))
+            nc.sync.dma_start(y_scale_rows[4 * q : 4 * q + 4], y_sc[32 * q : 32 * q + 4].bitcast(I32))

@@ -60,8 +60,9 @@ def tile_list_lineage_fitness_gradients_kernel(
             w1_raw[:].bitcast(I32).rearrange("p (a c) -> p a c", a=2),
             w1_words.bitcast(I32).rearrange("a p c -> p a c"),
         )
-        for q in range(4):
-            nc.sync.dma_start(tab_sc[32 * q : 32 * q + 8, :].bitcast(I32), tab_scales[:, 4 * q : 4 * q + 4, :].bitcast(I32))
+        tab_scale_rows = tab_scales.bitcast(I32).rearrange("a (q r) c -> r q a c", r=4)
+        for r in range(4):
+            nc.sync.dma_start(tab_sc[r:P:16, :].bitcast(I32), tab_scale_rows[r])
         load_tab(0)
         for q in range(4):
             nc.sync.dma_start(
@@ -90,7 +91,7 @@ def tile_list_lineage_fitness_gradients_kernel(
 
         v_sc = held([P, S], U8, "v_sc")
         nc.vector.tensor_copy(v_sc[:], tab_sc[:].indirect(offs_sb[:]))
-        nc.scalar.dma_start(v_sc1[0:100, :].bitcast(I32), v_sc[4:104, :].bitcast(I32))
+        nc.scalar.dma_start(v_sc1[0:100, :].bitcast(I32), v_sc[16:116, :].bitcast(I32))
         w1_w = held([P, 2 * 2 * H], U8, "w1_w")
         deal(w1_w[:].bitcast(U16), w1_raw[:].bitcast(U16), 8)
         w1_sc = held([P, 2 * H], U8, "w1_sc")
@@ -120,6 +121,15 @@ def tile_list_lineage_fitness_gradients_kernel(
                 stop=(a == 1),
             )
 
+        w2_w = [held([P, 512], U32, f"w2_w{b}") for b in range(2)]
+        w2_sc = [held([P, 512], U8, f"w2_sc{b}") for b in range(2)]
+        w2_bf = [held([P, 2048], BF16, f"w2_bf{b}") for b in range(2)]
+        w2_woven = [w2_bf[b][:].rearrange("p (t m j) -> p m t j", t=4, j=4) for b in range(2)]
+        w2_rows_in = [w2_raw[b][:].rearrange("p j (m t) -> p m t j", t=4) for b in range(2)]
+
+        def quantise_w2(b):
+            nc.vector.quantize_mx(out=w2_w[b][:].bitcast(FP8X4), scales=w2_sc[b][:], in_=w2_bf[b][:])
+
         order = [(0, 0), (1, 0), (0, 1), (1, 1)] + [(s, c) for s in range(2, 8) for c in range(2)]
         banks = {}
         for s, c in sorted(order[:6], key=lambda sc: sc[1]):
@@ -134,6 +144,8 @@ def tile_list_lineage_fitness_gradients_kernel(
                 th[s][:, c * BANK : (c + 1) * BANK], banks[(s, c)][:], ACT.Tanh,
                 bias=bias_sb[:, s // 4, s % 4 : s % 4 + 1],
             )
+            if (s, c) == (4, 1):
+                nc.scalar.activation(w2_woven[0], w2_rows_in[0], ACT.Copy, scale=-1.0)
 
         picked = {}
 
@@ -146,23 +158,6 @@ def tile_list_lineage_fitness_gradients_kernel(
             for n, i in enumerate(chunks):
                 picked[(i, b)] = tile[:, :, n * P : (n + 1) * P]
 
-        w2_w = [held([P, 512], U32, f"w2_w{b}") for b in range(2)]
-        w2_sc = [held([P, 512], U8, f"w2_sc{b}") for b in range(2)]
-
-        w2_both = held([P, 4096], BF16, "w2_both")
-
-        def quantise_w2(b):
-            w2_bf = w2_both[:, 2048 * b : 2048 * (b + 1)]
-            nc.gpsimd.tensor_scalar(
-                out=w2_bf.rearrange("p (t m j) -> p m t j", t=4, j=4),
-                in0=w2_raw[b][:].rearrange("p j (m t) -> p m t j", t=4),
-                scalar1=-1.0,
-                scalar2=0.0,
-                op0=ALU.mult,
-                op1=ALU.add,
-            )
-            nc.vector.quantize_mx(out=w2_w[b][:].bitcast(FP8X4), scales=w2_sc[b][:], in_=w2_bf)
-
         v2_w = held([P, M], U32, "v2_w")
         v2_sc = held([P, M], U8, "v2_sc")
         h_w = {}
@@ -172,7 +167,11 @@ def tile_list_lineage_fitness_gradients_kernel(
 
         def square(i, b, tag=None):
             sq[(i, b)] = held([P, P, 4], F32, f"sq{i}{b}", tag)
-            nc.scalar.activation(sq[(i, b)][:], picked[(i, b)].rearrange("p t m -> p m t"), ACT.Square)
+            nc.scalar.activation(
+                sq[(i, b)][:].rearrange("p (c i) t -> p c t i", i=4),
+                picked[(i, b)].rearrange("p t (c i) -> p c t i", i=4),
+                ACT.Square,
+            )
 
         def make_h(i, b):
             cols = slice(i * P, (i + 1) * P)
@@ -227,11 +226,12 @@ def tile_list_lineage_fitness_gradients_kernel(
                         start=(a == 0),
                         stop=(a == 1),
                     )
+            nc.scalar.copy(y_sb[:], bank[:])
             if i == CHUNKS - 1:
-                nc.vector.tensor_copy(y_bf[:], bank[:].rearrange("p t m -> p m t"))
-                nc.scalar.copy(y_sb[:], bank[:])
+                nc.vector.tensor_copy(
+                    y_bf[:].rearrange("p (c i) t -> p c t i", i=4), y_sb[:].rearrange("p t (c i) -> p c t i", i=4)
+                )
             else:
-                nc.scalar.copy(y_sb[:], bank[:])
                 nc.scalar.copy(y_bf[:], bank[:].rearrange("p t m -> p m t"))
             nc.sync.dma_start(y_rows[g][:, :, cols], y_sb[:])
             nc.vector.quantize_mx(
@@ -245,6 +245,7 @@ def tile_list_lineage_fitness_gradients_kernel(
         nc.vector.tensor_copy(v2_sc[:], tab2_sc[:].indirect(offs2_sb[:]))
         pick((0, 1), 1)
         quantise_w2(0)
+        nc.vector.tensor_scalar(out=w2_woven[1], in0=w2_rows_in[1], scalar1=-1.0, scalar2=None, op0=ALU.mult)
         quantise_w2(1)
         deal(w3_w[:], w3_raw[:], 4)
         deal(w3_sc[:], w3_sc_raw[:], 16)

@@ -27,7 +27,8 @@ def tile_list_lineage_fitness_gradients_kernel(
     nc = tc.nc
     with ExitStack() as ctx:
         keep = ctx.enter_context(tc.tile_pool(name="keep", bufs=1))
-        acc = ctx.enter_context(tc.psum_pool(name="acc", bufs=8))
+        acc = ctx.enter_context(tc.psum_pool(name="acc", bufs=5))
+        errs = ctx.enter_context(tc.psum_pool(name="errs", bufs=3))
 
         def held(shape, dtype, name, tag=None):
             return keep.tile(shape, dtype, name=name, tag=tag or name, align_bytes=64)
@@ -64,17 +65,16 @@ def tile_list_lineage_fitness_gradients_kernel(
         for r in range(4):
             nc.sync.dma_start(tab_sc[r:P:16, :].bitcast(I32), tab_scale_rows[r])
         load_tab(0)
-        for q in range(4):
-            nc.sync.dma_start(
-                w1_sc_raw[32 * q : 32 * q + 4, :].bitcast(I32).rearrange("r (a c) -> r a c", a=2),
-                w1_scales[:, 4 * q : 4 * q + 4, :].bitcast(I32).rearrange("a r c -> r a c"),
-            )
+        w1_scale_rows = w1_scales.bitcast(I32).rearrange("a (q r) c -> r q a c", r=4)
+        for r in range(4):
+            nc.sync.dma_start(w1_sc_raw[r:P:32, :].bitcast(I32).rearrange("q (a c) -> q a c", a=2), w1_scale_rows[r])
         nc.sync.dma_start(bias_sb[:], bias.rearrange("(b p t) -> p b t", b=2, t=4))
         load_tab(1)
         nc.sync.dma_start(tab2_w[:].bitcast(I32), tab2_words[0].rearrange("p n i -> p (n i)").bitcast(I32))
         nc.sync.dma_start(w2_raw[0][:], w2_rows[:, :, 0:512])
-        for q in range(4):
-            nc.sync.dma_start(tab2_sc[32 * q : 32 * q + 4, :].bitcast(I32), tab2_scales[0, 4 * q : 4 * q + 4, :].bitcast(I32))
+        tab2_scale_rows = tab2_scales[0].bitcast(I32).rearrange("(q r) c -> r q c", r=4)
+        for r in range(4):
+            nc.sync.dma_start(tab2_sc[r:P:32, :].bitcast(I32), tab2_scale_rows[r])
         nc.sync.dma_start(w2_raw[1][:], w2_rows[:, :, 512:1024])
         nc.sync.dma_start(
             w3_raw[:].rearrange("p (a c) -> p a c", a=2),
@@ -132,7 +132,7 @@ def tile_list_lineage_fitness_gradients_kernel(
 
         order = [(0, 0), (1, 0), (0, 1), (1, 1)] + [(s, c) for s in range(2, 8) for c in range(2)]
         banks = {}
-        for s, c in sorted(order[:6], key=lambda sc: sc[1]):
+        for s, c in sorted(order[:5], key=lambda sc: sc[1]):
             banks[(s, c)] = acc.tile([P, BANK], F32, name="bank")
             pre_pass(banks[(s, c)], s, c, 0)
         for s, c in order:
@@ -160,8 +160,9 @@ def tile_list_lineage_fitness_gradients_kernel(
 
         v2_w = held([P, M], U32, "v2_w")
         v2_sc = held([P, M], U8, "v2_sc")
-        h_w = {}
-        h_sc = {}
+        h_bf = [held([P, 2 * BANK], BF16, f"h_bf{i}") for i in range(CHUNKS)]
+        h_w = [held([P, 2 * P], U32, f"h_w{i}") for i in range(CHUNKS)]
+        h_sc = [held([P, 2 * P], U8, f"h_sc{i}") for i in range(CHUNKS)]
 
         sq = {}
 
@@ -175,7 +176,7 @@ def tile_list_lineage_fitness_gradients_kernel(
 
         def make_h(i, b):
             cols = slice(i * P, (i + 1) * P)
-            err = acc.tile([P, 4, P], F32, name="bank")
+            err = errs.tile([P, 4, P], F32, name="err")
             for t in range(4):
                 nc.tensor.matmul_mx(
                     out=err[:, t, :],
@@ -186,23 +187,19 @@ def tile_list_lineage_fitness_gradients_kernel(
                     start=True,
                     stop=True,
                 )
-            h_bf = held([P, P, 4], BF16, f"h_bf{i}{b}")
             nc.vector.scalar_tensor_tensor(
-                out=h_bf[:],
+                out=h_bf[i][:, b * BANK : (b + 1) * BANK].rearrange("p (m t) -> p m t", t=4),
                 in0=sq[(i, b)][:],
                 scalar=1.0,
                 in1=err[:].rearrange("p t m -> p m t"),
                 op0=ALU.subtract,
                 op1=ALU.mult,
             )
-            h_w[(i, b)] = held([P, P], U32, f"h_w{i}{b}")
-            h_sc[(i, b)] = held([P, P], U8, f"h_sc{i}{b}")
-            nc.vector.quantize_mx(
-                out=h_w[(i, b)][:].bitcast(FP8X4), scales=h_sc[(i, b)][:], in_=h_bf[:].rearrange("p m t -> p (m t)")
-            )
+            if b == 1:
+                nc.vector.quantize_mx(out=h_w[i][:].bitcast(FP8X4), scales=h_sc[i][:], in_=h_bf[i][:])
 
-        w3_w = held([P, 2 * N], I32, "w3_w")
-        w3_sc = held([P, N], U8, "w3_sc")
+        w3_w = held([P, 2 * N], I32, "w3_w", "w1_w")
+        w3_sc = held([P, N], U8, "w3_sc", "w1_sc")
         y_sc = held([P, 2, M], U8, "y_sc")
         y_rows = out_0.rearrange("(g p t) m -> g p t m", g=2, t=4)
         y_words = out_1.rearrange("g p m i -> g p (m i)").bitcast(I32).rearrange("g p m -> p g m")
@@ -221,13 +218,13 @@ def tile_list_lineage_fitness_gradients_kernel(
                         out=bank[:, t, :],
                         lhsT=w3_w[:, a * N + col : a * N + col + P].bitcast(FP8X4),
                         lhsT_scale=w3_sc[4 * a : P, col : col + P],
-                        rhs=h_w[(i, a)][:].bitcast(FP8X4),
-                        rhs_scale=h_sc[(i, a)][:],
+                        rhs=h_w[i][:, a * P : (a + 1) * P].bitcast(FP8X4),
+                        rhs_scale=h_sc[i][:, a * P : (a + 1) * P],
                         start=(a == 0),
                         stop=(a == 1),
                     )
             nc.scalar.copy(y_sb[:], bank[:])
-            if i == CHUNKS - 1:
+            if i >= CHUNKS // 2:
                 nc.vector.tensor_copy(
                     y_bf[:].rearrange("p (c i) t -> p c t i", i=4), y_sb[:].rearrange("p t (c i) -> p c t i", i=4)
                 )
@@ -237,32 +234,31 @@ def tile_list_lineage_fitness_gradients_kernel(
             nc.vector.quantize_mx(
                 out=y_w[i][:, g, :].bitcast(FP8X4), scales=y_sc[:, g, cols], in_=y_bf[:].rearrange("p m t -> p (m t)")
             )
-            if g == 1:
+            if i == CHUNKS - 1:
+                nc.sync.dma_start(y_words[:, g, cols], y_w[i][:, g, :].bitcast(I32))
+            elif g == 1:
                 nc.sync.dma_start(y_words[:, :, cols], y_w[i][:].bitcast(I32))
 
         nc.vector.tensor_copy(v2_w[:], tab2_w[:].indirect(offs2_sb[:]))
-        pick((0, 1), 0)
+        pick((0, 1, 2, 3), 0)
         nc.vector.tensor_copy(v2_sc[:], tab2_sc[:].indirect(offs2_sb[:]))
         pick((0, 1), 1)
         quantise_w2(0)
-        nc.vector.tensor_scalar(out=w2_woven[1], in0=w2_rows_in[1], scalar1=-1.0, scalar2=None, op0=ALU.mult)
+        nc.scalar.activation(w2_woven[1], w2_rows_in[1], ACT.Copy, scale=-1.0)
         quantise_w2(1)
         deal(w3_w[:], w3_raw[:], 4)
         deal(w3_sc[:], w3_sc_raw[:], 16)
-        square(0, 0, "w1_sc")
-        make_h(0, 0)
-        square(0, 1)
-        make_h(0, 1)
-        square(1, 0, "w1_w")
-        square(1, 1)
-        make_h(1, 0)
-        make_h(1, 1)
-        for i in (2, 3):
-            pick((i,), 0, f"sq{i - 2}1")
-            pick((i,), 1, f"h_bf{i - 2}1")
+        for i in (0, 1):
             for b in range(2):
-                make_y(i - 2, b)
                 square(i, b)
+        for i in (0, 1):
+            for b in range(2):
+                make_h(i, b)
+        for i in (2, 3):
+            pick((i,), 1, f"sq{i - 2}1")
+            for b in range(2):
+                square(i, b)
+                make_y(i - 2, b)
             for b in range(2):
                 make_h(i, b)
         for i in (2, 3):
@@ -270,4 +266,4 @@ def tile_list_lineage_fitness_gradients_kernel(
                 make_y(i, g)
         y_scale_rows = out_2.bitcast(I32).rearrange("g q m -> q g m")
         for q in range(4):
-            nc.sync.dma_start(y_scale_rows[4 * q : 4 * q + 4], y_sc[32 * q : 32 * q + 4].bitcast(I32))
+            nc.scalar.dma_start(y_scale_rows[4 * q : 4 * q + 4], y_sc[32 * q : 32 * q + 4].bitcast(I32))

@@ -17,6 +17,8 @@ P = 128
 K, K2, H, N, T, T2, S, M = 1024, 512, 1024, 1024, 4096, 2048, 1024, 512
 BANK = 512
 CHUNKS = 4
+SCALAR_ROUNDS = 5
+OPENED_EARLY = 8
 FLOPS = 2 * (K * H * S + K2 * H * M + H * N * M)
 
 
@@ -27,8 +29,7 @@ def tile_list_lineage_fitness_gradients_kernel(
     nc = tc.nc
     with ExitStack() as ctx:
         keep = ctx.enter_context(tc.tile_pool(name="keep", bufs=1))
-        acc = ctx.enter_context(tc.psum_pool(name="acc", bufs=5))
-        errs = ctx.enter_context(tc.psum_pool(name="errs", bufs=3))
+        acc = ctx.enter_context(tc.psum_pool(name="acc", bufs=8))
 
         def held(shape, dtype, name, tag=None):
             return keep.tile(shape, dtype, name=name, tag=tag or name, align_bytes=64)
@@ -40,9 +41,12 @@ def tile_list_lineage_fitness_gradients_kernel(
         v_sc1 = held([P, S], U8, "v_sc1")
         w1_sc_raw = held([P, 2 * H], U8, "w1_sc_raw")
         tab2_sc = held([P, T2], U8, "tab2_sc")
-        w3_sc_raw = held([P, N], U8, "w3_sc_raw")
-        for plane in (tab_sc, w1_sc_raw, v_sc1, tab2_sc, w3_sc_raw):
+        v2_sc = held([P, M], U8, "v2_sc")
+        w3_sc = held([P, 2 * N], U8, "w3_sc")
+        for plane in (tab_sc, w1_sc_raw):
             nc.vector.memset(plane[:].bitcast(I32), 0)
+        for plane in (tab2_sc, v_sc1, v2_sc, w3_sc):
+            nc.gpsimd.memset(plane[:].bitcast(I32), 0)
         w1_raw = held([P, 2 * 2 * H], U8, "w1_raw")
         tab_w = [held([P, T], U32, f"tab_w{a}") for a in range(2)]
         bias_sb = held([P, 2, 4], F32, "bias_sb")
@@ -51,12 +55,14 @@ def tile_list_lineage_fitness_gradients_kernel(
         w3_raw = held([P, 2 * N], I32, "w3_raw")
         w2_rows = w2.rearrange("(p j) r -> p j r", j=4)
 
-        def load_tab(a):
-            nc.sync.dma_start(tab_w[a][:].bitcast(I32), tab_words[a].rearrange("p n i -> p (n i)").bitcast(I32))
+        def load_tab(a, cols):
+            words = tab_words[a].rearrange("p n i -> p (n i)").bitcast(I32)
+            nc.sync.dma_start(tab_w[a][:].bitcast(I32)[:, cols], words[:, cols])
 
         nc.sync.dma_start(offs_sb[:], offs)
         nc.sync.dma_start(offs2_sb[:], offs2)
         nc.sync.dma_start(pos_sb[:], pos1)
+        nc.sync.dma_start(bias_sb[:], bias.rearrange("(b p t) -> p b t", b=2, t=4))
         nc.sync.dma_start(
             w1_raw[:].bitcast(I32).rearrange("p (a c) -> p a c", a=2),
             w1_words.bitcast(I32).rearrange("a p c -> p a c"),
@@ -64,24 +70,19 @@ def tile_list_lineage_fitness_gradients_kernel(
         tab_scale_rows = tab_scales.bitcast(I32).rearrange("a (q r) c -> r q a c", r=4)
         for r in range(4):
             nc.sync.dma_start(tab_sc[r:P:16, :].bitcast(I32), tab_scale_rows[r])
-        load_tab(0)
+        nc.sync.dma_start(tab2_sc[0:P:8, :].bitcast(I32), tab2_scales[0].bitcast(I32))
+        nc.sync.dma_start(
+            w1_sc_raw[4:P:8, :].bitcast(I32).rearrange("q (a c) -> q a c", a=2),
+            w3_scales.bitcast(I32).rearrange("a q c -> q a c"),
+        )
+        load_tab(0, slice(0, T // 2))
         w1_scale_rows = w1_scales.bitcast(I32).rearrange("a (q r) c -> r q a c", r=4)
         for r in range(4):
             nc.sync.dma_start(w1_sc_raw[r:P:32, :].bitcast(I32).rearrange("q (a c) -> q a c", a=2), w1_scale_rows[r])
-        nc.sync.dma_start(bias_sb[:], bias.rearrange("(b p t) -> p b t", b=2, t=4))
-        load_tab(1)
+        load_tab(0, slice(T // 2, T))
+        load_tab(1, slice(0, T))
         nc.sync.dma_start(tab2_w[:].bitcast(I32), tab2_words[0].rearrange("p n i -> p (n i)").bitcast(I32))
         nc.sync.dma_start(w2_raw[0][:], w2_rows[:, :, 0:512])
-        tab2_scale_rows = tab2_scales[0].bitcast(I32).rearrange("(q r) c -> r q c", r=4)
-        for r in range(4):
-            nc.sync.dma_start(tab2_sc[r:P:32, :].bitcast(I32), tab2_scale_rows[r])
-        nc.sync.dma_start(w2_raw[1][:], w2_rows[:, :, 512:1024])
-        nc.sync.dma_start(
-            w3_raw[:].rearrange("p (a c) -> p a c", a=2),
-            w3_words.rearrange("a p n i -> a p (n i)").bitcast(I32).rearrange("a p c -> p a c"),
-        )
-        for q in range(4):
-            nc.sync.dma_start(w3_sc_raw[32 * q : 32 * q + 8, :].bitcast(I32), w3_scales[:, 4 * q : 4 * q + 4, :].bitcast(I32))
 
         def deal(dst, src, run):
             nc.vector.tensor_copy(
@@ -94,17 +95,28 @@ def tile_list_lineage_fitness_gradients_kernel(
         nc.scalar.dma_start(v_sc1[0:100, :].bitcast(I32), v_sc[16:116, :].bitcast(I32))
         w1_w = held([P, 2 * 2 * H], U8, "w1_w")
         deal(w1_w[:].bitcast(U16), w1_raw[:].bitcast(U16), 8)
+        v2_sc_rows = held([P, M], U8, "v2_sc_rows")
+        nc.vector.tensor_copy(v2_sc_rows[:], tab2_sc[:].indirect(offs2_sb[:]))
         w1_sc = held([P, 2 * H], U8, "w1_sc")
         v_w = [[held([P, BANK], U32, f"v_w{a}{c}") for c in range(2)] for a in range(2)]
 
         def look_up(a, c):
             nc.vector.tensor_copy(v_w[a][c][:], tab_w[a][:].indirect(offs_sb[:, 32 * c : 32 * (c + 1)]))
 
+        deal(w1_sc[:], w1_sc_raw[:], 16)
         for c in range(2):
             look_up(0, c)
-            deal(w1_sc[:, c * H : (c + 1) * H], w1_sc_raw[:, c * H : (c + 1) * H], 16)
         for c in range(2):
             look_up(1, c)
+        nc.sync.dma_start(w2_raw[1][:], w2_rows[:, :, 512:1024])
+        nc.sync.dma_start(
+            w3_raw[:].rearrange("p (a c) -> p a c", a=2),
+            w3_words.rearrange("a p n i -> a p (n i)").bitcast(I32).rearrange("a p c -> p a c"),
+        )
+        for q in range(4):
+            nc.sync.dma_start(v2_sc[32 * q + 4 : 32 * q + 8, :].bitcast(I32), v2_sc_rows[32 * q : 32 * q + 32 : 8, :].bitcast(I32))
+        for q in range(4):
+            nc.sync.dma_start(w3_sc[32 * q + 8 : 32 * q + 12, :].bitcast(I32), w1_sc[32 * q + 4 : 32 * q + 32 : 8, :].bitcast(I32))
         v_planes = [v_sc, v_sc1]
 
         th = [held([P, S], F32, f"th{s}") for s in range(8)]
@@ -132,7 +144,7 @@ def tile_list_lineage_fitness_gradients_kernel(
 
         order = [(0, 0), (1, 0), (0, 1), (1, 1)] + [(s, c) for s in range(2, 8) for c in range(2)]
         banks = {}
-        for s, c in sorted(order[:5], key=lambda sc: sc[1]):
+        for s, c in sorted(order[:OPENED_EARLY], key=lambda sc: sc[1]):
             banks[(s, c)] = acc.tile([P, BANK], F32, name="bank")
             pre_pass(banks[(s, c)], s, c, 0)
         for s, c in order:
@@ -144,8 +156,6 @@ def tile_list_lineage_fitness_gradients_kernel(
                 th[s][:, c * BANK : (c + 1) * BANK], banks[(s, c)][:], ACT.Tanh,
                 bias=bias_sb[:, s // 4, s % 4 : s % 4 + 1],
             )
-            if (s, c) == (4, 1):
-                nc.scalar.activation(w2_woven[0], w2_rows_in[0], ACT.Copy, scale=-1.0)
 
         picked = {}
 
@@ -159,7 +169,6 @@ def tile_list_lineage_fitness_gradients_kernel(
                 picked[(i, b)] = tile[:, :, n * P : (n + 1) * P]
 
         v2_w = held([P, M], U32, "v2_w")
-        v2_sc = held([P, M], U8, "v2_sc")
         h_bf = [held([P, 2 * BANK], BF16, f"h_bf{i}") for i in range(CHUNKS)]
         h_w = [held([P, 2 * P], U32, f"h_w{i}") for i in range(CHUNKS)]
         h_sc = [held([P, 2 * P], U8, f"h_sc{i}") for i in range(CHUNKS)]
@@ -176,14 +185,14 @@ def tile_list_lineage_fitness_gradients_kernel(
 
         def make_h(i, b):
             cols = slice(i * P, (i + 1) * P)
-            err = errs.tile([P, 4, P], F32, name="err")
+            err = acc.tile([P, 4, P], F32, name="bank")
             for t in range(4):
                 nc.tensor.matmul_mx(
                     out=err[:, t, :],
                     lhsT=w2_w[b][:, t * P : (t + 1) * P].bitcast(FP8X4),
                     lhsT_scale=w2_sc[b][:, t * P : (t + 1) * P],
                     rhs=v2_w[:, cols].bitcast(FP8X4),
-                    rhs_scale=v2_sc[:, cols],
+                    rhs_scale=v2_sc[4:P, cols],
                     start=True,
                     stop=True,
                 )
@@ -195,75 +204,118 @@ def tile_list_lineage_fitness_gradients_kernel(
                 op0=ALU.subtract,
                 op1=ALU.mult,
             )
-            if b == 1:
-                nc.vector.quantize_mx(out=h_w[i][:].bitcast(FP8X4), scales=h_sc[i][:], in_=h_bf[i][:])
+
+        def quantise_h(i, b):
+            cols = slice(b * P, (b + 1) * P)
+            nc.vector.quantize_mx(
+                out=h_w[i][:, cols].bitcast(FP8X4), scales=h_sc[i][:, cols], in_=h_bf[i][:, b * BANK : (b + 1) * BANK]
+            )
 
         w3_w = held([P, 2 * N], I32, "w3_w", "w1_w")
-        w3_sc = held([P, N], U8, "w3_sc", "w1_sc")
         y_sc = held([P, 2, M], U8, "y_sc")
         y_rows = out_0.rearrange("(g p t) m -> g p t m", g=2, t=4)
         y_words = out_1.rearrange("g p m i -> g p (m i)").bitcast(I32).rearrange("g p m -> p g m")
 
         y_w = [held([P, 2, P], U32, f"y_w{i}") for i in range(CHUNKS)]
 
-        def make_y(i, g):
-            cols = slice(i * P, (i + 1) * P)
-            y_sb = held([P, 4, P], F32, f"y_sb{i}{g}")
-            y_bf = held([P, P, 4], BF16, f"y_bf{i}{g}")
-            bank = acc.tile([P, 4, P], F32, name="bank")
+        y_bank, y_sb, y_bf = {}, {}, {}
+
+        def y_passes(i, g, a):
+            if a == 0:
+                y_bank[(i, g)] = acc.tile([P, 4, P], F32, name="bank")
             for t in range(4):
                 col = (4 * g + t) * P
-                for a in range(2):
-                    nc.tensor.matmul_mx(
-                        out=bank[:, t, :],
-                        lhsT=w3_w[:, a * N + col : a * N + col + P].bitcast(FP8X4),
-                        lhsT_scale=w3_sc[4 * a : P, col : col + P],
-                        rhs=h_w[i][:, a * P : (a + 1) * P].bitcast(FP8X4),
-                        rhs_scale=h_sc[i][:, a * P : (a + 1) * P],
-                        start=(a == 0),
-                        stop=(a == 1),
-                    )
-            nc.scalar.copy(y_sb[:], bank[:])
-            if i >= CHUNKS // 2:
-                nc.vector.tensor_copy(
-                    y_bf[:].rearrange("p (c i) t -> p c t i", i=4), y_sb[:].rearrange("p t (c i) -> p c t i", i=4)
+                nc.tensor.matmul_mx(
+                    out=y_bank[(i, g)][:, t, :],
+                    lhsT=w3_w[:, a * N + col : a * N + col + P].bitcast(FP8X4),
+                    lhsT_scale=w3_sc[8:P, a * N + col : a * N + col + P],
+                    rhs=h_w[i][:, a * P : (a + 1) * P].bitcast(FP8X4),
+                    rhs_scale=h_sc[i][:, a * P : (a + 1) * P],
+                    start=(a == 0 and t == 0),
+                    stop=(a == 1 and t == 3),
                 )
-            else:
-                nc.scalar.copy(y_bf[:], bank[:].rearrange("p t m -> p m t"))
-            nc.sync.dma_start(y_rows[g][:, :, cols], y_sb[:])
+
+        def store_y(i, g):
+            y_sb[(i, g)] = held([P, 4, P], F32, f"y_sb{i}{g}")
+            nc.scalar.copy(y_sb[(i, g)][:], y_bank[(i, g)][:])
+            nc.sync.dma_start(y_rows[g][:, :, i * P : (i + 1) * P], y_sb[(i, g)][:])
+
+        def round_y(i, g, copy):
+            y_bf[(i, g)] = held([P, P, 4], BF16, f"y_bf{i}{g}")
+            copy(y_bf[(i, g)][:], y_bank[(i, g)][:].rearrange("p t m -> p m t"))
+
+        def round_stored_y(i, g):
+            y_bf[(i, g)] = held([P, P, 4], BF16, f"y_bf{i}{g}")
+            nc.vector.tensor_copy(
+                y_bf[(i, g)][:].rearrange("p (c i) t -> p c t i", i=4),
+                y_sb[(i, g)][:].rearrange("p t (c i) -> p c t i", i=4),
+            )
+
+        def quantise_y(i, g):
+            cols = slice(i * P, (i + 1) * P)
             nc.vector.quantize_mx(
-                out=y_w[i][:, g, :].bitcast(FP8X4), scales=y_sc[:, g, cols], in_=y_bf[:].rearrange("p m t -> p (m t)")
+                out=y_w[i][:, g, :].bitcast(FP8X4),
+                scales=y_sc[:, g, cols],
+                in_=y_bf[(i, g)][:].rearrange("p m t -> p (m t)"),
             )
             if i == CHUNKS - 1:
                 nc.sync.dma_start(y_words[:, g, cols], y_w[i][:, g, :].bitcast(I32))
             elif g == 1:
                 nc.sync.dma_start(y_words[:, :, cols], y_w[i][:].bitcast(I32))
 
+        def make_y(i, g):
+            for a in range(2):
+                y_passes(i, g, a)
+            store_y(i, g)
+            if 2 * i + g < SCALAR_ROUNDS:
+                round_y(i, g, nc.scalar.copy)
+            else:
+                round_stored_y(i, g)
+            quantise_y(i, g)
+
+        def finish_h(i):
+            for b in range(2):
+                make_h(i, b)
+            for b in range(2):
+                quantise_h(i, b)
+
         nc.vector.tensor_copy(v2_w[:], tab2_w[:].indirect(offs2_sb[:]))
+        nc.vector.tensor_scalar_mul(w2_woven[0], w2_rows_in[0], -1.0)
         pick((0, 1, 2, 3), 0)
-        nc.vector.tensor_copy(v2_sc[:], tab2_sc[:].indirect(offs2_sb[:]))
-        pick((0, 1), 1)
         quantise_w2(0)
         nc.scalar.activation(w2_woven[1], w2_rows_in[1], ACT.Copy, scale=-1.0)
-        quantise_w2(1)
         deal(w3_w[:], w3_raw[:], 4)
-        deal(w3_sc[:], w3_sc_raw[:], 16)
+        pick((0, 1), 1)
+        quantise_w2(1)
         for i in (0, 1):
             for b in range(2):
                 square(i, b)
         for i in (0, 1):
-            for b in range(2):
-                make_h(i, b)
-        for i in (2, 3):
-            pick((i,), 1, f"sq{i - 2}1")
-            for b in range(2):
-                square(i, b)
-                make_y(i - 2, b)
-            for b in range(2):
-                make_h(i, b)
-        for i in (2, 3):
+            finish_h(i)
+        pick((2,), 1, "sq01")
+        square(2, 0)
+        make_y(0, 0)
+        square(2, 1)
+        pick((3,), 1, "sq11")
+        finish_h(2)
+        make_y(0, 1)
+        square(3, 0)
+        make_y(1, 0)
+        square(3, 1)
+        finish_h(3)
+        make_y(1, 1)
+        for g in range(2):
+            make_y(2, g)
+        last = CHUNKS - 1
+        for a in range(2):
             for g in range(2):
-                make_y(i, g)
+                y_passes(last, g, a)
+        store_y(last, 0)
+        round_y(last, 1, nc.vector.tensor_copy)
+        store_y(last, 1)
+        round_stored_y(last, 0)
+        quantise_y(last, 1)
+        quantise_y(last, 0)
         y_scale_rows = out_2.bitcast(I32).rearrange("g q m -> q g m")
         for q in range(4):
             nc.scalar.dma_start(y_scale_rows[4 * q : 4 * q + 4], y_sc[32 * q : 32 * q + 4].bitcast(I32))

@@ -17,7 +17,8 @@ P = 128
 K, K2, H, N, T, T2, S, M = 1024, 512, 1024, 1024, 4096, 2048, 1024, 512
 BANK = 512
 CHUNKS = 4
-SCALAR_ROUNDS = 5
+SCALAR_ROUNDS = ((3, 1),)
+WORD_STORES = {(3, 0): (slice(0, 1), 0), (3, 1): (slice(1, 2), 0)}
 OPENED_EARLY = 8
 FLOPS = 2 * (K * H * S + K2 * H * M + H * N * M)
 
@@ -38,14 +39,14 @@ def tile_list_lineage_fitness_gradients_kernel(
         pos_sb = keep.tile([P, M // 16], U16, name="pos_sb")
         offs2_sb = keep.tile([P, M // 16], U16, name="offs2_sb")
         tab_sc = held([P, T], U8, "tab_sc")
-        v_sc1 = held([P, S], U8, "v_sc1")
+        v_sc = held([P, 2 * S], U8, "v_sc")
         w1_sc_raw = held([P, 2 * H], U8, "w1_sc_raw")
         tab2_sc = held([P, T2], U8, "tab2_sc")
         v2_sc = held([P, M], U8, "v2_sc")
         w3_sc = held([P, 2 * N], U8, "w3_sc")
         for plane in (tab_sc, w1_sc_raw):
             nc.vector.memset(plane[:].bitcast(I32), 0)
-        for plane in (tab2_sc, v_sc1, v2_sc, w3_sc):
+        for plane in (tab2_sc, v_sc, v2_sc, w3_sc):
             nc.gpsimd.memset(plane[:].bitcast(I32), 0)
         w1_raw = held([P, 2 * 2 * H], U8, "w1_raw")
         tab_w = [held([P, T], U32, f"tab_w{a}") for a in range(2)]
@@ -60,26 +61,28 @@ def tile_list_lineage_fitness_gradients_kernel(
             nc.sync.dma_start(tab_w[a][:].bitcast(I32)[:, cols], words[:, cols])
 
         nc.sync.dma_start(offs_sb[:], offs)
-        nc.sync.dma_start(offs2_sb[:], offs2)
-        nc.sync.dma_start(pos_sb[:], pos1)
-        nc.sync.dma_start(bias_sb[:], bias.rearrange("(b p t) -> p b t", b=2, t=4))
         nc.sync.dma_start(
             w1_raw[:].bitcast(I32).rearrange("p (a c) -> p a c", a=2),
             w1_words.bitcast(I32).rearrange("a p c -> p a c"),
         )
-        tab_scale_rows = tab_scales.bitcast(I32).rearrange("a (q r) c -> r q a c", r=4)
-        for r in range(4):
-            nc.sync.dma_start(tab_sc[r:P:16, :].bitcast(I32), tab_scale_rows[r])
+        nc.sync.dma_start(tab_sc[0:P:4, :].bitcast(I32), tab_scales.bitcast(I32).rearrange("a q c -> q a c"))
+        nc.sync.dma_start(offs2_sb[:], offs2)
         nc.sync.dma_start(tab2_sc[0:P:8, :].bitcast(I32), tab2_scales[0].bitcast(I32))
         nc.sync.dma_start(
             w1_sc_raw[4:P:8, :].bitcast(I32).rearrange("q (a c) -> q a c", a=2),
             w3_scales.bitcast(I32).rearrange("a q c -> q a c"),
         )
+        nc.sync.dma_start(pos_sb[:], pos1)
+        nc.sync.dma_start(bias_sb[:], bias.rearrange("(b p t) -> p b t", b=2, t=4))
         load_tab(0, slice(0, T // 2))
         w1_scale_rows = w1_scales.bitcast(I32).rearrange("a (q r) c -> r q a c", r=4)
         for r in range(4):
             nc.sync.dma_start(w1_sc_raw[r:P:32, :].bitcast(I32).rearrange("q (a c) -> q a c", a=2), w1_scale_rows[r])
         load_tab(0, slice(T // 2, T))
+        v_sc_rows = held([P, S], U8, "v_sc_rows")
+        nc.vector.tensor_copy(v_sc_rows[:], tab_sc[:].indirect(offs_sb[:]))
+        for q in range(4):
+            nc.sync.dma_start(v_sc[32 * q : 32 * q + 4, :].bitcast(I32), v_sc_rows[32 * q : 32 * q + 32 : 4, :].bitcast(I32))
         load_tab(1, slice(0, T))
         nc.sync.dma_start(tab2_w[:].bitcast(I32), tab2_words[0].rearrange("p n i -> p (n i)").bitcast(I32))
         nc.sync.dma_start(w2_raw[0][:], w2_rows[:, :, 0:512])
@@ -90,13 +93,10 @@ def tile_list_lineage_fitness_gradients_kernel(
                 in_=src.rearrange("p (g u i t) -> p g u t i", t=4, u=P // run, i=run),
             )
 
-        v_sc = held([P, S], U8, "v_sc")
-        nc.vector.tensor_copy(v_sc[:], tab_sc[:].indirect(offs_sb[:]))
-        nc.scalar.dma_start(v_sc1[0:100, :].bitcast(I32), v_sc[16:116, :].bitcast(I32))
-        w1_w = held([P, 2 * 2 * H], U8, "w1_w")
-        deal(w1_w[:].bitcast(U16), w1_raw[:].bitcast(U16), 8)
+        w1_w = held([P, 2 * 2 * H], U8, "w1_w", "tab_sc")
         v2_sc_rows = held([P, M], U8, "v2_sc_rows")
         nc.vector.tensor_copy(v2_sc_rows[:], tab2_sc[:].indirect(offs2_sb[:]))
+        deal(w1_w[:].bitcast(U16), w1_raw[:].bitcast(U16), 8)
         w1_sc = held([P, 2 * H], U8, "w1_sc")
         v_w = [[held([P, BANK], U32, f"v_w{a}{c}") for c in range(2)] for a in range(2)]
 
@@ -117,7 +117,6 @@ def tile_list_lineage_fitness_gradients_kernel(
             nc.sync.dma_start(v2_sc[32 * q + 4 : 32 * q + 8, :].bitcast(I32), v2_sc_rows[32 * q : 32 * q + 32 : 8, :].bitcast(I32))
         for q in range(4):
             nc.sync.dma_start(w3_sc[32 * q + 8 : 32 * q + 12, :].bitcast(I32), w1_sc[32 * q + 4 : 32 * q + 32 : 8, :].bitcast(I32))
-        v_planes = [v_sc, v_sc1]
 
         th = [held([P, S], F32, f"th{s}") for s in range(8)]
 
@@ -128,7 +127,7 @@ def tile_list_lineage_fitness_gradients_kernel(
                 lhsT=w1_w[:, 2 * col : 2 * (col + P)].bitcast(FP4X4),
                 lhsT_scale=w1_sc[:, col : col + P],
                 rhs=v_w[a][c][:].bitcast(FP8X4),
-                rhs_scale=v_planes[a][:, c * BANK : (c + 1) * BANK],
+                rhs_scale=v_sc[:, a * S + c * BANK : a * S + (c + 1) * BANK],
                 start=(a == 0),
                 stop=(a == 1),
             )
@@ -138,6 +137,7 @@ def tile_list_lineage_fitness_gradients_kernel(
         w2_bf = [held([P, 2048], BF16, f"w2_bf{b}") for b in range(2)]
         w2_woven = [w2_bf[b][:].rearrange("p (t m j) -> p m t j", t=4, j=4) for b in range(2)]
         w2_rows_in = [w2_raw[b][:].rearrange("p j (m t) -> p m t j", t=4) for b in range(2)]
+        w2_by_line = [view[1].rearrange("p m t j -> p m j t") for view in (w2_woven, w2_rows_in)]
 
         def quantise_w2(b):
             nc.vector.quantize_mx(out=w2_w[b][:].bitcast(FP8X4), scales=w2_sc[b][:], in_=w2_bf[b][:])
@@ -211,12 +211,12 @@ def tile_list_lineage_fitness_gradients_kernel(
                 out=h_w[i][:, cols].bitcast(FP8X4), scales=h_sc[i][:, cols], in_=h_bf[i][:, b * BANK : (b + 1) * BANK]
             )
 
-        w3_w = held([P, 2 * N], I32, "w3_w", "w1_w")
+        w3_w = held([P, 2 * N], I32, "w3_w", "tab_sc")
         y_sc = held([P, 2, M], U8, "y_sc")
         y_rows = out_0.rearrange("(g p t) m -> g p t m", g=2, t=4)
         y_words = out_1.rearrange("g p m i -> g p (m i)").bitcast(I32).rearrange("g p m -> p g m")
 
-        y_w = [held([P, 2, P], U32, f"y_w{i}") for i in range(CHUNKS)]
+        y_w = held([P, 2, M], U32, "y_w")
 
         y_bank, y_sb, y_bf = {}, {}, {}
 
@@ -254,20 +254,20 @@ def tile_list_lineage_fitness_gradients_kernel(
         def quantise_y(i, g):
             cols = slice(i * P, (i + 1) * P)
             nc.vector.quantize_mx(
-                out=y_w[i][:, g, :].bitcast(FP8X4),
+                out=y_w[:, g, cols].bitcast(FP8X4),
                 scales=y_sc[:, g, cols],
                 in_=y_bf[(i, g)][:].rearrange("p m t -> p (m t)"),
             )
-            if i == CHUNKS - 1:
-                nc.sync.dma_start(y_words[:, g, cols], y_w[i][:, g, :].bitcast(I32))
-            elif g == 1:
-                nc.sync.dma_start(y_words[:, :, cols], y_w[i][:].bitcast(I32))
+            if (i, g) in WORD_STORES:
+                gs, first = WORD_STORES[(i, g)]
+                cols = slice(first * P, (i + 1) * P)
+                nc.sync.dma_start(y_words[:, gs, cols], y_w[:].bitcast(I32)[:, gs, cols])
 
         def make_y(i, g):
             for a in range(2):
                 y_passes(i, g, a)
             store_y(i, g)
-            if 2 * i + g < SCALAR_ROUNDS:
+            if (i, g) in SCALAR_ROUNDS:
                 round_y(i, g, nc.scalar.copy)
             else:
                 round_stored_y(i, g)
@@ -283,39 +283,45 @@ def tile_list_lineage_fitness_gradients_kernel(
         nc.vector.tensor_scalar_mul(w2_woven[0], w2_rows_in[0], -1.0)
         pick((0, 1, 2, 3), 0)
         quantise_w2(0)
-        nc.scalar.activation(w2_woven[1], w2_rows_in[1], ACT.Copy, scale=-1.0)
+        nc.scalar.activation(w2_by_line[0], w2_by_line[1], ACT.Copy, scale=-1.0)
         deal(w3_w[:], w3_raw[:], 4)
-        pick((0, 1), 1)
+        pick((0, 1, 2), 1)
         quantise_w2(1)
-        for i in (0, 1):
-            for b in range(2):
-                square(i, b)
-        for i in (0, 1):
-            finish_h(i)
-        pick((2,), 1, "sq01")
-        square(2, 0)
-        make_y(0, 0)
-        square(2, 1)
-        pick((3,), 1, "sq11")
+
+        def sum_and_store(i, g):
+            for a in range(2):
+                y_passes(i, g, a)
+            store_y(i, g)
+
+        def planes(i, g):
+            if (i, g) in SCALAR_ROUNDS:
+                round_y(i, g, nc.scalar.copy)
+            else:
+                round_stored_y(i, g)
+            quantise_y(i, g)
+
+        for i, b in ((0, 0), (1, 0), (0, 1), (1, 1), (2, 0), (2, 1)):
+            square(i, b)
+        for i, b in ((0, 0), (1, 0), (0, 1)):
+            make_h(i, b)
+        quantise_h(0, 0)
+        quantise_h(0, 1)
+        make_h(1, 1)
+        quantise_h(1, 0)
+        pick((3,), 1, "sq01")
+        quantise_h(1, 1)
         finish_h(2)
-        make_y(0, 1)
+        sum_and_store(0, 0)
         square(3, 0)
-        make_y(1, 0)
+        sum_and_store(0, 1)
         square(3, 1)
         finish_h(3)
-        make_y(1, 1)
-        for g in range(2):
-            make_y(2, g)
-        last = CHUNKS - 1
-        for a in range(2):
+        for i in (1, 2, 3):
             for g in range(2):
-                y_passes(last, g, a)
-        store_y(last, 0)
-        round_y(last, 1, nc.vector.tensor_copy)
-        store_y(last, 1)
-        round_stored_y(last, 0)
-        quantise_y(last, 1)
-        quantise_y(last, 0)
+                sum_and_store(i, g)
+        for i in range(CHUNKS):
+            for g in range(2):
+                planes(i, g)
         y_scale_rows = out_2.bitcast(I32).rearrange("g q m -> q g m")
         for q in range(4):
             nc.scalar.dma_start(y_scale_rows[4 * q : 4 * q + 4], y_sc[32 * q : 32 * q + 4].bitcast(I32))

@@ -67,7 +67,7 @@ def tile_list_lineage_fitness_gradients_kernel(
         )
         nc.sync.dma_start(tab_sc[0:P:4, :].bitcast(I32), tab_scales.bitcast(I32).rearrange("a q c -> q a c"))
         nc.sync.dma_start(offs2_sb[:], offs2)
-        nc.sync.dma_start(tab2_sc[0:P:8, :].bitcast(I32), tab2_scales[0].bitcast(I32))
+        nc.sync.dma_start(tab2_sc[4:P:8, :].bitcast(I32), tab2_scales[0].bitcast(I32))
         nc.sync.dma_start(
             w1_sc_raw[4:P:8, :].bitcast(I32).rearrange("q (a c) -> q a c", a=2),
             w3_scales.bitcast(I32).rearrange("a q c -> q a c"),
@@ -114,7 +114,7 @@ def tile_list_lineage_fitness_gradients_kernel(
             w3_words.rearrange("a p n i -> a p (n i)").bitcast(I32).rearrange("a p c -> p a c"),
         )
         for q in range(4):
-            nc.sync.dma_start(v2_sc[32 * q + 4 : 32 * q + 8, :].bitcast(I32), v2_sc_rows[32 * q : 32 * q + 32 : 8, :].bitcast(I32))
+            nc.sync.dma_start(v2_sc[32 * q + 4 : 32 * q + 8, :].bitcast(I32), v2_sc_rows[32 * q + 4 : 32 * q + 32 : 8, :].bitcast(I32))
         for q in range(4):
             nc.sync.dma_start(w3_sc[32 * q + 8 : 32 * q + 12, :].bitcast(I32), w1_sc[32 * q + 4 : 32 * q + 32 : 8, :].bitcast(I32))
 
@@ -137,7 +137,7 @@ def tile_list_lineage_fitness_gradients_kernel(
         w2_bf = [held([P, 2048], BF16, f"w2_bf{b}") for b in range(2)]
         w2_woven = [w2_bf[b][:].rearrange("p (t m j) -> p m t j", t=4, j=4) for b in range(2)]
         w2_rows_in = [w2_raw[b][:].rearrange("p j (m t) -> p m t j", t=4) for b in range(2)]
-        w2_by_line = [view[1].rearrange("p m t j -> p m j t") for view in (w2_woven, w2_rows_in)]
+        w2_by_line = [[view[b].rearrange("p m t j -> p m j t") for view in (w2_woven, w2_rows_in)] for b in range(2)]
 
         def quantise_w2(b):
             nc.vector.quantize_mx(out=w2_w[b][:].bitcast(FP8X4), scales=w2_sc[b][:], in_=w2_bf[b][:])
@@ -241,13 +241,11 @@ def tile_list_lineage_fitness_gradients_kernel(
             nc.sync.dma_start(y_rows[g][:, :, i * P : (i + 1) * P], y_sb[(i, g)][:])
 
         def round_y(i, g, copy):
-            y_bf[(i, g)] = held([P, P, 4], BF16, f"y_bf{i}{g}")
-            copy(y_bf[(i, g)][:], y_bank[(i, g)][:].rearrange("p t m -> p m t"))
+            copy(y_bf[(i, g)], y_bank[(i, g)][:].rearrange("p t m -> p m t"))
 
         def round_stored_y(i, g):
-            y_bf[(i, g)] = held([P, P, 4], BF16, f"y_bf{i}{g}")
             nc.vector.tensor_copy(
-                y_bf[(i, g)][:].rearrange("p (c i) t -> p c t i", i=4),
+                y_bf[(i, g)].rearrange("p (c i) t -> p c t i", i=4),
                 y_sb[(i, g)][:].rearrange("p t (c i) -> p c t i", i=4),
             )
 
@@ -256,7 +254,7 @@ def tile_list_lineage_fitness_gradients_kernel(
             nc.vector.quantize_mx(
                 out=y_w[:, g, cols].bitcast(FP8X4),
                 scales=y_sc[:, g, cols],
-                in_=y_bf[(i, g)][:].rearrange("p m t -> p (m t)"),
+                in_=y_bf[(i, g)].rearrange("p m t -> p (m t)"),
             )
             if (i, g) in WORD_STORES:
                 gs, first = WORD_STORES[(i, g)]
@@ -280,11 +278,13 @@ def tile_list_lineage_fitness_gradients_kernel(
                 quantise_h(i, b)
 
         nc.vector.tensor_copy(v2_w[:], tab2_w[:].indirect(offs2_sb[:]))
-        nc.vector.tensor_scalar_mul(w2_woven[0], w2_rows_in[0], -1.0)
+        nc.vector.tensor_scalar_mul(w2_by_line[0][0], w2_by_line[0][1], -1.0)
         pick((0, 1, 2, 3), 0)
         quantise_w2(0)
-        nc.scalar.activation(w2_by_line[0], w2_by_line[1], ACT.Copy, scale=-1.0)
-        deal(w3_w[:], w3_raw[:], 4)
+        nc.scalar.activation(w2_by_line[1][0], w2_by_line[1][1], ACT.Copy, scale=-1.0)
+        nc.vector.tensor_copy(
+            out=w3_w[:].rearrange("p (g t m) -> p g m t", t=4, m=P), in_=w3_raw[:].rearrange("p (g m t) -> p g m t", t=4, m=P)
+        )
         pick((0, 1, 2), 1)
         quantise_w2(1)
 
@@ -304,23 +304,26 @@ def tile_list_lineage_fitness_gradients_kernel(
             square(i, b)
         for i, b in ((0, 0), (1, 0), (0, 1)):
             make_h(i, b)
-        quantise_h(0, 0)
-        quantise_h(0, 1)
+        for i, b in ((0, 0), (1, 0), (0, 1)):
+            quantise_h(i, b)
         make_h(1, 1)
-        quantise_h(1, 0)
         pick((3,), 1, "sq01")
         quantise_h(1, 1)
         finish_h(2)
         sum_and_store(0, 0)
         square(3, 0)
         sum_and_store(0, 1)
-        square(3, 1)
+        for g in range(2):
+            sum_and_store(1, g)
+        square(3, 1, "h_bf1")
         finish_h(3)
-        for i in (1, 2, 3):
+        for i in (2, 3):
             for g in range(2):
                 sum_and_store(i, g)
+        y_rounded = held([P, 2 * CHUNKS, P, 4], BF16, "y_rounded", "sq01")
         for i in range(CHUNKS):
             for g in range(2):
+                y_bf[(i, g)] = y_rounded[:, 2 * i + g]
                 planes(i, g)
         y_scale_rows = out_2.bitcast(I32).rearrange("g q m -> q g m")
         for q in range(4):

@@ -17,7 +17,7 @@ P = 128
 K, K2, H, N, T, T2, S, M = 1024, 512, 1024, 1024, 4096, 2048, 1024, 512
 BANK = 512
 CHUNKS = 4
-SCALAR_ROUNDS = ((3, 1),)
+SCALAR_ROUNDS = ((2, 1), (3, 1))
 WORD_STORES = {(3, 0): (slice(0, 1), 0), (3, 1): (slice(1, 2), 0)}
 OPENED_EARLY = 8
 FLOPS = 2 * (K * H * S + K2 * H * M + H * N * M)
@@ -44,10 +44,8 @@ def tile_list_lineage_fitness_gradients_kernel(
         tab2_sc = held([P, T2], U8, "tab2_sc")
         v2_sc = held([P, M], U8, "v2_sc")
         w3_sc = held([P, 2 * N], U8, "w3_sc")
-        for plane in (tab_sc, w1_sc_raw):
+        for plane in (tab_sc, tab2_sc, w1_sc_raw, v_sc, v2_sc, w3_sc):
             nc.vector.memset(plane[:].bitcast(I32), 0)
-        for plane in (tab2_sc, v_sc, v2_sc, w3_sc):
-            nc.gpsimd.memset(plane[:].bitcast(I32), 0)
         w1_raw = held([P, 2 * 2 * H], U8, "w1_raw")
         tab_w = [held([P, T], U32, f"tab_w{a}") for a in range(2)]
         bias_sb = held([P, 2, 4], F32, "bias_sb")

@@ -17,7 +17,7 @@ P = 128
 K, K2, H, N, T, T2, S, M = 1024, 512, 1024, 1024, 4096, 2048, 1024, 512
 BANK = 512
 CHUNKS = 4
-SCALAR_ROUNDS = ((2, 1), (3, 1))
+SCALAR_ROUNDS = ((1, 1), (2, 1), (3, 1))
 WORD_STORES = {(3, 0): (slice(0, 1), 0), (3, 1): (slice(1, 2), 0)}
 OPENED_EARLY = 8
 FLOPS = 2 * (K * H * S + K2 * H * M + H * N * M)
@@ -77,11 +77,12 @@ def tile_list_lineage_fitness_gradients_kernel(
         for r in range(4):
             nc.sync.dma_start(w1_sc_raw[r:P:32, :].bitcast(I32).rearrange("q (a c) -> q a c", a=2), w1_scale_rows[r])
         load_tab(0, slice(T // 2, T))
+        load_tab(1, slice(0, T // 4))
         v_sc_rows = held([P, S], U8, "v_sc_rows")
         nc.vector.tensor_copy(v_sc_rows[:], tab_sc[:].indirect(offs_sb[:]))
         for q in range(4):
             nc.sync.dma_start(v_sc[32 * q : 32 * q + 4, :].bitcast(I32), v_sc_rows[32 * q : 32 * q + 32 : 4, :].bitcast(I32))
-        load_tab(1, slice(0, T))
+        load_tab(1, slice(T // 4, T))
         nc.sync.dma_start(tab2_w[:].bitcast(I32), tab2_words[0].rearrange("p n i -> p (n i)").bitcast(I32))
         nc.sync.dma_start(w2_raw[0][:], w2_rows[:, :, 0:512])
 

@@ -16,10 +16,12 @@ ALU = mybir.AluOpType
 P = 128
 K, K2, H, N, T, T2, S, M = 1024, 512, 1024, 1024, 4096, 2048, 1024, 512
 BANK = 512
-CHUNKS = 4
-SCALAR_ROUNDS = ((1, 1), (2, 1), (3, 1))
-WORD_STORES = {(3, 0): (slice(0, 1), 0), (3, 1): (slice(1, 2), 0)}
-OPENED_EARLY = 8
+BANKS = 8
+CHUNKS = M // P
+LAST = CHUNKS - 1
+V2_FIRST, W3_FIRST = 4, 8
+AHEAD = T // 4
+SCALAR_ROUNDS = ((LAST - 1, 1), (LAST, 1))
 FLOPS = 2 * (K * H * S + K2 * H * M + H * N * M)
 
 
@@ -30,22 +32,35 @@ def tile_list_lineage_fitness_gradients_kernel(
     nc = tc.nc
     with ExitStack() as ctx:
         keep = ctx.enter_context(tc.tile_pool(name="keep", bufs=1))
-        acc = ctx.enter_context(tc.psum_pool(name="acc", bufs=8))
+        acc = ctx.enter_context(tc.psum_pool(name="acc", bufs=BANKS))
 
-        def held(shape, dtype, name, tag=None):
-            return keep.tile(shape, dtype, name=name, tag=tag or name, align_bytes=64)
+        def held(shape, dtype, name, after=None):
+            return keep.tile(shape, dtype, name=name, tag=after or name, align_bytes=64)
+
+        def move_rows(plane, first, rows, start, step):
+            for quad in range(0, P, 32):
+                nc.sync.dma_start(
+                    plane[quad + first : quad + first + 4, :].bitcast(I32),
+                    rows[quad + start : quad + 32 : step, :].bitcast(I32),
+                )
+
+        def deal(dst, src, run):
+            nc.vector.tensor_copy(
+                out=dst.rearrange("p (g t u i) -> p g u t i", t=4, u=P // run, i=run),
+                in_=src.rearrange("p (g u i t) -> p g u t i", t=4, u=P // run, i=run),
+            )
 
         offs_sb = keep.tile([P, S // 16], U16, name="offs_sb")
         pos_sb = keep.tile([P, M // 16], U16, name="pos_sb")
         offs2_sb = keep.tile([P, M // 16], U16, name="offs2_sb")
         tab_sc = held([P, T], U8, "tab_sc")
         v_sc = held([P, 2 * S], U8, "v_sc")
-        w1_sc_raw = held([P, 2 * H], U8, "w1_sc_raw")
+        weight_sc_raw = held([P, 2 * H], U8, "weight_sc_raw")
         tab2_sc = held([P, T2], U8, "tab2_sc")
         v2_sc = held([P, M], U8, "v2_sc")
         w3_sc = held([P, 2 * N], U8, "w3_sc")
-        for plane in (tab_sc, tab2_sc, w1_sc_raw, v_sc, v2_sc, w3_sc):
-            nc.vector.memset(plane[:].bitcast(I32), 0)
+        for scale_tile in (tab_sc, tab2_sc, weight_sc_raw, v_sc, v2_sc, w3_sc):
+            nc.vector.memset(scale_tile[:].bitcast(I32), 0)
         w1_raw = held([P, 2 * 2 * H], U8, "w1_raw")
         tab_w = [held([P, T], U32, f"tab_w{a}") for a in range(2)]
         bias_sb = held([P, 2, 4], F32, "bias_sb")
@@ -65,57 +80,46 @@ def tile_list_lineage_fitness_gradients_kernel(
         )
         nc.sync.dma_start(tab_sc[0:P:4, :].bitcast(I32), tab_scales.bitcast(I32).rearrange("a q c -> q a c"))
         nc.sync.dma_start(offs2_sb[:], offs2)
-        nc.sync.dma_start(tab2_sc[4:P:8, :].bitcast(I32), tab2_scales[0].bitcast(I32))
-        nc.sync.dma_start(
-            w1_sc_raw[4:P:8, :].bitcast(I32).rearrange("q (a c) -> q a c", a=2),
-            w3_scales.bitcast(I32).rearrange("a q c -> q a c"),
-        )
         nc.sync.dma_start(pos_sb[:], pos1)
         nc.sync.dma_start(bias_sb[:], bias.rearrange("(b p t) -> p b t", b=2, t=4))
         load_tab(0, slice(0, T // 2))
+        nc.sync.dma_start(tab2_sc[4:P:8, :].bitcast(I32), tab2_scales[0].bitcast(I32))
+        nc.sync.dma_start(
+            weight_sc_raw[4:P:8, :].bitcast(I32).rearrange("q (a c) -> q a c", a=2),
+            w3_scales.bitcast(I32).rearrange("a q c -> q a c"),
+        )
         w1_scale_rows = w1_scales.bitcast(I32).rearrange("a (q r) c -> r q a c", r=4)
         for r in range(4):
-            nc.sync.dma_start(w1_sc_raw[r:P:32, :].bitcast(I32).rearrange("q (a c) -> q a c", a=2), w1_scale_rows[r])
+            nc.sync.dma_start(
+                weight_sc_raw[r:P:32, :].bitcast(I32).rearrange("q (a c) -> q a c", a=2), w1_scale_rows[r]
+            )
         load_tab(0, slice(T // 2, T))
-        load_tab(1, slice(0, T // 4))
+        load_tab(1, slice(0, AHEAD))
         v_sc_rows = held([P, S], U8, "v_sc_rows")
         nc.vector.tensor_copy(v_sc_rows[:], tab_sc[:].indirect(offs_sb[:]))
-        for q in range(4):
-            nc.sync.dma_start(v_sc[32 * q : 32 * q + 4, :].bitcast(I32), v_sc_rows[32 * q : 32 * q + 32 : 4, :].bitcast(I32))
-        load_tab(1, slice(T // 4, T))
+        move_rows(v_sc, 0, v_sc_rows, 0, 4)
+        load_tab(1, slice(AHEAD, T))
         nc.sync.dma_start(tab2_w[:].bitcast(I32), tab2_words[0].rearrange("p n i -> p (n i)").bitcast(I32))
         nc.sync.dma_start(w2_raw[0][:], w2_rows[:, :, 0:512])
 
-        def deal(dst, src, run):
-            nc.vector.tensor_copy(
-                out=dst.rearrange("p (g t u i) -> p g u t i", t=4, u=P // run, i=run),
-                in_=src.rearrange("p (g u i t) -> p g u t i", t=4, u=P // run, i=run),
-            )
-
-        w1_w = held([P, 2 * 2 * H], U8, "w1_w", "tab_sc")
+        w1_w = held([P, 2 * 2 * H], U8, "w1_w")
         v2_sc_rows = held([P, M], U8, "v2_sc_rows")
         nc.vector.tensor_copy(v2_sc_rows[:], tab2_sc[:].indirect(offs2_sb[:]))
         deal(w1_w[:].bitcast(U16), w1_raw[:].bitcast(U16), 8)
-        w1_sc = held([P, 2 * H], U8, "w1_sc")
+        weight_sc = held([P, 2 * H], U8, "weight_sc")
         v_w = [[held([P, BANK], U32, f"v_w{a}{c}") for c in range(2)] for a in range(2)]
+        deal(weight_sc[:], weight_sc_raw[:], 16)
+        for a in range(2):
+            for c in range(2):
+                nc.vector.tensor_copy(v_w[a][c][:], tab_w[a][:].indirect(offs_sb[:, 32 * c : 32 * (c + 1)]))
 
-        def look_up(a, c):
-            nc.vector.tensor_copy(v_w[a][c][:], tab_w[a][:].indirect(offs_sb[:, 32 * c : 32 * (c + 1)]))
-
-        deal(w1_sc[:], w1_sc_raw[:], 16)
-        for c in range(2):
-            look_up(0, c)
-        for c in range(2):
-            look_up(1, c)
         nc.sync.dma_start(w2_raw[1][:], w2_rows[:, :, 512:1024])
         nc.sync.dma_start(
             w3_raw[:].rearrange("p (a c) -> p a c", a=2),
             w3_words.rearrange("a p n i -> a p (n i)").bitcast(I32).rearrange("a p c -> p a c"),
         )
-        for q in range(4):
-            nc.sync.dma_start(v2_sc[32 * q + 4 : 32 * q + 8, :].bitcast(I32), v2_sc_rows[32 * q + 4 : 32 * q + 32 : 8, :].bitcast(I32))
-        for q in range(4):
-            nc.sync.dma_start(w3_sc[32 * q + 8 : 32 * q + 12, :].bitcast(I32), w1_sc[32 * q + 4 : 32 * q + 32 : 8, :].bitcast(I32))
+        move_rows(v2_sc, V2_FIRST, v2_sc_rows, 4, 8)
+        move_rows(w3_sc, W3_FIRST, weight_sc, 4, 8)
 
         th = [held([P, S], F32, f"th{s}") for s in range(8)]
 
@@ -124,7 +128,7 @@ def tile_list_lineage_fitness_gradients_kernel(
             nc.tensor.matmul_mx(
                 out=bank[:],
                 lhsT=w1_w[:, 2 * col : 2 * (col + P)].bitcast(FP4X4),
-                lhsT_scale=w1_sc[:, col : col + P],
+                lhsT_scale=weight_sc[:, col : col + P],
                 rhs=v_w[a][c][:].bitcast(FP8X4),
                 rhs_scale=v_sc[:, a * S + c * BANK : a * S + (c + 1) * BANK],
                 start=(a == 0),
@@ -134,48 +138,43 @@ def tile_list_lineage_fitness_gradients_kernel(
         w2_w = [held([P, 512], U32, f"w2_w{b}") for b in range(2)]
         w2_sc = [held([P, 512], U8, f"w2_sc{b}") for b in range(2)]
         w2_bf = [held([P, 2048], BF16, f"w2_bf{b}") for b in range(2)]
-        w2_woven = [w2_bf[b][:].rearrange("p (t m j) -> p m t j", t=4, j=4) for b in range(2)]
-        w2_rows_in = [w2_raw[b][:].rearrange("p j (m t) -> p m t j", t=4) for b in range(2)]
-        w2_by_line = [[view[b].rearrange("p m t j -> p m j t") for view in (w2_woven, w2_rows_in)] for b in range(2)]
+        w2_dealt = [w2_bf[b][:].rearrange("p (t m j) -> p m j t", t=4, j=4) for b in range(2)]
+        w2_lines = [w2_raw[b][:].rearrange("p j (m t) -> p m j t", t=4) for b in range(2)]
 
         def quantise_w2(b):
             nc.vector.quantize_mx(out=w2_w[b][:].bitcast(FP8X4), scales=w2_sc[b][:], in_=w2_bf[b][:])
 
         order = [(0, 0), (1, 0), (0, 1), (1, 1)] + [(s, c) for s in range(2, 8) for c in range(2)]
-        banks = {}
-        for s, c in sorted(order[:OPENED_EARLY], key=lambda sc: sc[1]):
-            banks[(s, c)] = acc.tile([P, BANK], F32, name="bank")
-            pre_pass(banks[(s, c)], s, c, 0)
+        pre_bank = {}
+        for s, c in sorted(order[:BANKS], key=lambda sc: sc[1]):
+            pre_bank[(s, c)] = acc.tile([P, BANK], F32, name="bank")
+            pre_pass(pre_bank[(s, c)], s, c, 0)
         for s, c in order:
-            if (s, c) not in banks:
-                banks[(s, c)] = acc.tile([P, BANK], F32, name="bank")
-                pre_pass(banks[(s, c)], s, c, 0)
-            pre_pass(banks[(s, c)], s, c, 1)
+            if (s, c) not in pre_bank:
+                pre_bank[(s, c)] = acc.tile([P, BANK], F32, name="bank")
+                pre_pass(pre_bank[(s, c)], s, c, 0)
+            pre_pass(pre_bank[(s, c)], s, c, 1)
             nc.scalar.activation(
-                th[s][:, c * BANK : (c + 1) * BANK], banks[(s, c)][:], ACT.Tanh,
+                th[s][:, c * BANK : (c + 1) * BANK], pre_bank[(s, c)][:], ACT.Tanh,
                 bias=bias_sb[:, s // 4, s % 4 : s % 4 + 1],
             )
 
-        picked = {}
+        picked, sq = {}, {}
 
-        def pick(chunks, b, tag=None):
-            width = len(chunks) * P
-            tile = held([P, 4, width], F32, f"picked{chunks[0]}{b}", tag)
-            offsets = pos_sb[:, 8 * chunks[0] : 8 * (chunks[-1] + 1)]
+        def pick(first, last, b, after=None):
+            tile = held([P, 4, (last + 1 - first) * P], F32, f"picked{first}{b}", after)
             for t in range(4):
-                nc.vector.tensor_copy(tile[:, t, :], th[4 * b + t][:].indirect(offsets))
-            for n, i in enumerate(chunks):
-                picked[(i, b)] = tile[:, :, n * P : (n + 1) * P]
+                nc.vector.tensor_copy(tile[:, t, :], th[4 * b + t][:].indirect(pos_sb[:, 8 * first : 8 * (last + 1)]))
+            for i in range(first, last + 1):
+                picked[(i, b)] = tile[:, :, (i - first) * P : (i + 1 - first) * P]
 
         v2_w = held([P, M], U32, "v2_w")
         h_bf = [held([P, 2 * BANK], BF16, f"h_bf{i}") for i in range(CHUNKS)]
         h_w = [held([P, 2 * P], U32, f"h_w{i}") for i in range(CHUNKS)]
         h_sc = [held([P, 2 * P], U8, f"h_sc{i}") for i in range(CHUNKS)]
 
-        sq = {}
-
-        def square(i, b, tag=None):
-            sq[(i, b)] = held([P, P, 4], F32, f"sq{i}{b}", tag)
+        def square(i, b, after=None):
+            sq[(i, b)] = held([P, P, 4], F32, f"sq{i}{b}", after)
             nc.scalar.activation(
                 sq[(i, b)][:].rearrange("p (c i) t -> p c t i", i=4),
                 picked[(i, b)].rearrange("p t (c i) -> p c t i", i=4),
@@ -184,14 +183,14 @@ def tile_list_lineage_fitness_gradients_kernel(
 
         def make_h(i, b):
             cols = slice(i * P, (i + 1) * P)
-            err = acc.tile([P, 4, P], F32, name="bank")
+            minus_err = acc.tile([P, 4, P], F32, name="bank")
             for t in range(4):
                 nc.tensor.matmul_mx(
-                    out=err[:, t, :],
+                    out=minus_err[:, t, :],
                     lhsT=w2_w[b][:, t * P : (t + 1) * P].bitcast(FP8X4),
                     lhsT_scale=w2_sc[b][:, t * P : (t + 1) * P],
                     rhs=v2_w[:, cols].bitcast(FP8X4),
-                    rhs_scale=v2_sc[4:P, cols],
+                    rhs_scale=v2_sc[V2_FIRST:P, cols],
                     start=True,
                     stop=True,
                 )
@@ -199,7 +198,7 @@ def tile_list_lineage_fitness_gradients_kernel(
                 out=h_bf[i][:, b * BANK : (b + 1) * BANK].rearrange("p (m t) -> p m t", t=4),
                 in0=sq[(i, b)][:],
                 scalar=1.0,
-                in1=err[:].rearrange("p t m -> p m t"),
+                in1=minus_err[:].rearrange("p t m -> p m t"),
                 op0=ALU.subtract,
                 op1=ALU.mult,
             )
@@ -210,120 +209,90 @@ def tile_list_lineage_fitness_gradients_kernel(
                 out=h_w[i][:, cols].bitcast(FP8X4), scales=h_sc[i][:, cols], in_=h_bf[i][:, b * BANK : (b + 1) * BANK]
             )
 
-        w3_w = held([P, 2 * N], I32, "w3_w", "tab_sc")
-        y_sc = held([P, 2, M], U8, "y_sc")
-        y_rows = out_0.rearrange("(g p t) m -> g p t m", g=2, t=4)
-        y_words = out_1.rearrange("g p m i -> g p (m i)").bitcast(I32).rearrange("g p m -> p g m")
-
-        y_w = held([P, 2, M], U32, "y_w")
-
-        y_bank, y_sb, y_bf = {}, {}, {}
-
-        def y_passes(i, g, a):
-            if a == 0:
-                y_bank[(i, g)] = acc.tile([P, 4, P], F32, name="bank")
-            for t in range(4):
-                col = (4 * g + t) * P
-                nc.tensor.matmul_mx(
-                    out=y_bank[(i, g)][:, t, :],
-                    lhsT=w3_w[:, a * N + col : a * N + col + P].bitcast(FP8X4),
-                    lhsT_scale=w3_sc[8:P, a * N + col : a * N + col + P],
-                    rhs=h_w[i][:, a * P : (a + 1) * P].bitcast(FP8X4),
-                    rhs_scale=h_sc[i][:, a * P : (a + 1) * P],
-                    start=(a == 0 and t == 0),
-                    stop=(a == 1 and t == 3),
-                )
-
-        def store_y(i, g):
-            y_sb[(i, g)] = held([P, 4, P], F32, f"y_sb{i}{g}")
-            nc.scalar.copy(y_sb[(i, g)][:], y_bank[(i, g)][:])
-            nc.sync.dma_start(y_rows[g][:, :, i * P : (i + 1) * P], y_sb[(i, g)][:])
-
-        def round_y(i, g, copy):
-            copy(y_bf[(i, g)], y_bank[(i, g)][:].rearrange("p t m -> p m t"))
-
-        def round_stored_y(i, g):
-            nc.vector.tensor_copy(
-                y_bf[(i, g)].rearrange("p (c i) t -> p c t i", i=4),
-                y_sb[(i, g)][:].rearrange("p t (c i) -> p c t i", i=4),
-            )
-
-        def quantise_y(i, g):
-            cols = slice(i * P, (i + 1) * P)
-            nc.vector.quantize_mx(
-                out=y_w[:, g, cols].bitcast(FP8X4),
-                scales=y_sc[:, g, cols],
-                in_=y_bf[(i, g)].rearrange("p m t -> p (m t)"),
-            )
-            if (i, g) in WORD_STORES:
-                gs, first = WORD_STORES[(i, g)]
-                cols = slice(first * P, (i + 1) * P)
-                nc.sync.dma_start(y_words[:, gs, cols], y_w[:].bitcast(I32)[:, gs, cols])
-
-        def make_y(i, g):
-            for a in range(2):
-                y_passes(i, g, a)
-            store_y(i, g)
-            if (i, g) in SCALAR_ROUNDS:
-                round_y(i, g, nc.scalar.copy)
-            else:
-                round_stored_y(i, g)
-            quantise_y(i, g)
-
         def finish_h(i):
             for b in range(2):
                 make_h(i, b)
             for b in range(2):
                 quantise_h(i, b)
 
-        nc.vector.tensor_copy(v2_w[:], tab2_w[:].indirect(offs2_sb[:]))
-        nc.vector.tensor_scalar_mul(w2_by_line[0][0], w2_by_line[0][1], -1.0)
-        pick((0, 1, 2, 3), 0)
-        quantise_w2(0)
-        nc.scalar.activation(w2_by_line[1][0], w2_by_line[1][1], ACT.Copy, scale=-1.0)
-        nc.vector.tensor_copy(
-            out=w3_w[:].rearrange("p (g t m) -> p g m t", t=4, m=P), in_=w3_raw[:].rearrange("p (g m t) -> p g m t", t=4, m=P)
-        )
-        pick((0, 1, 2), 1)
-        quantise_w2(1)
+        w3_w = held([P, 2 * N], I32, "w3_w", "w1_w")
+        y_sc = held([P, 2, M], U8, "y_sc")
+        y_w = held([P, 2, M], U32, "y_w")
+        y_rows = out_0.rearrange("(g p t) m -> g p t m", g=2, t=4)
+        y_words = out_1.rearrange("g p m i -> g p (m i)").bitcast(I32).rearrange("g p m -> p g m")
+        y_bank, y_sb = {}, {}
 
         def sum_and_store(i, g):
-            for a in range(2):
-                y_passes(i, g, a)
-            store_y(i, g)
+            y_bank[(i, g)] = acc.tile([P, 4, P], F32, name="bank")
+            for b in range(2):
+                for t in range(4):
+                    col = b * N + (4 * g + t) * P
+                    nc.tensor.matmul_mx(
+                        out=y_bank[(i, g)][:, t, :],
+                        lhsT=w3_w[:, col : col + P].bitcast(FP8X4),
+                        lhsT_scale=w3_sc[W3_FIRST:P, col : col + P],
+                        rhs=h_w[i][:, b * P : (b + 1) * P].bitcast(FP8X4),
+                        rhs_scale=h_sc[i][:, b * P : (b + 1) * P],
+                        start=(b == 0 and t == 0),
+                        stop=(b == 1 and t == 3),
+                    )
+            y_sb[(i, g)] = held([P, 4, P], F32, f"y_sb{i}{g}")
+            nc.scalar.copy(y_sb[(i, g)][:], y_bank[(i, g)][:])
+            nc.sync.dma_start(y_rows[g][:, :, i * P : (i + 1) * P], y_sb[(i, g)][:])
 
-        def planes(i, g):
+        def quantise_y(i, g, woven):
             if (i, g) in SCALAR_ROUNDS:
-                round_y(i, g, nc.scalar.copy)
+                nc.scalar.copy(woven, y_bank[(i, g)][:].rearrange("p t m -> p m t"))
             else:
-                round_stored_y(i, g)
-            quantise_y(i, g)
+                nc.vector.tensor_copy(
+                    woven.rearrange("p (c i) t -> p c t i", i=4),
+                    y_sb[(i, g)][:].rearrange("p t (c i) -> p c t i", i=4),
+                )
+            cols = slice(i * P, (i + 1) * P)
+            nc.vector.quantize_mx(
+                out=y_w[:, g, cols].bitcast(FP8X4), scales=y_sc[:, g, cols], in_=woven.rearrange("p m t -> p (m t)")
+            )
+            if i == LAST:
+                nc.sync.dma_start(y_words[:, g : g + 1, :], y_w[:].bitcast(I32)[:, g : g + 1, :])
 
-        for i, b in ((0, 0), (1, 0), (0, 1), (1, 1), (2, 0), (2, 1)):
+        nc.vector.tensor_copy(v2_w[:], tab2_w[:].indirect(offs2_sb[:]))
+        nc.vector.tensor_scalar_mul(w2_dealt[0], w2_lines[0], -1.0)
+        pick(0, LAST, 0)
+        quantise_w2(0)
+        nc.scalar.activation(w2_dealt[1], w2_lines[1], ACT.Copy, scale=-1.0)
+        nc.vector.tensor_copy(
+            out=w3_w[:].rearrange("p (g t m) -> p g m t", t=4, m=P),
+            in_=w3_raw[:].rearrange("p (g m t) -> p g m t", t=4, m=P),
+        )
+        pick(0, LAST - 1, 1)
+        quantise_w2(1)
+        opening = ((0, 0), (1, 0), (0, 1))
+        for i, b in opening + ((1, 1), (2, 0), (2, 1)):
             square(i, b)
-        for i, b in ((0, 0), (1, 0), (0, 1)):
+        for i, b in opening:
             make_h(i, b)
-        for i, b in ((0, 0), (1, 0), (0, 1)):
+        for i, b in opening:
             quantise_h(i, b)
         make_h(1, 1)
-        pick((3,), 1, "sq01")
+        pick(LAST, LAST, 1, "sq01")
         quantise_h(1, 1)
         finish_h(2)
         sum_and_store(0, 0)
-        square(3, 0)
+        square(LAST, 0)
         sum_and_store(0, 1)
         for g in range(2):
             sum_and_store(1, g)
-        square(3, 1, "h_bf1")
-        finish_h(3)
-        for i in (2, 3):
+        square(LAST, 1, "h_bf1")
+        finish_h(LAST)
+        for i in (LAST - 1, LAST):
             for g in range(2):
                 sum_and_store(i, g)
-        y_rounded = held([P, 2 * CHUNKS, P, 4], BF16, "y_rounded", "sq01")
+        y_bf = held([P, 2 * CHUNKS, P, 4], BF16, "y_bf", "sq01")
         for i in range(CHUNKS):
             for g in range(2):
-                y_bf[(i, g)] = y_rounded[:, 2 * i + g]
-                planes(i, g)
+                quantise_y(i, g, y_bf[:, 2 * i + g])
         y_scale_rows = out_2.bitcast(I32).rearrange("g q m -> q g m")
-        for q in range(4):
-            nc.scalar.dma_start(y_scale_rows[4 * q : 4 * q + 4], y_sc[32 * q : 32 * q + 4].bitcast(I32))
+        for quad in range(4):
+            nc.scalar.dma_start(
+                y_scale_rows[4 * quad : 4 * quad + 4], y_sc[32 * quad : 32 * quad + 4].bitcast(I32)
+            )

@@ -21,7 +21,7 @@ CHUNKS = M // P
 LAST = CHUNKS - 1
 V2_FIRST, W3_FIRST = 4, 8
 AHEAD = T // 4
-SCALAR_ROUNDS = ((LAST - 1, 1), (LAST, 1))
+SCALAR_ROUNDS = ((LAST - 1, 0), (LAST - 1, 1), (LAST, 1))
 FLOPS = 2 * (K * H * S + K2 * H * M + H * N * M)
 
 
@@ -135,11 +135,11 @@ def tile_list_lineage_fitness_gradients_kernel(
                 stop=(a == 1),
             )
 
-        w2_w = [held([P, 512], U32, f"w2_w{b}") for b in range(2)]
+        w2_w = [held([P, 512], U32, "w2_w0", "th2"), held([P, 512], U32, "w2_w1")]
         w2_sc = [held([P, 512], U8, f"w2_sc{b}") for b in range(2)]
-        w2_bf = [held([P, 2048], BF16, f"w2_bf{b}") for b in range(2)]
-        w2_dealt = [w2_bf[b][:].rearrange("p (t m j) -> p m j t", t=4, j=4) for b in range(2)]
-        w2_lines = [w2_raw[b][:].rearrange("p j (m t) -> p m j t", t=4) for b in range(2)]
+        w2_bf = [held([P, 2048], BF16, f"w2_bf{b}", "w2_bf0") for b in range(2)]
+        w2_dealt = [w2_bf[b][:].rearrange("p (t m j) -> p m t j", t=4, j=4) for b in range(2)]
+        w2_lines = [w2_raw[b][:].rearrange("p j (m t) -> p m t j", t=4) for b in range(2)]
 
         def quantise_w2(b):
             nc.vector.quantize_mx(out=w2_w[b][:].bitcast(FP8X4), scales=w2_sc[b][:], in_=w2_bf[b][:])
@@ -161,10 +161,12 @@ def tile_list_lineage_fitness_gradients_kernel(
 
         picked, sq = {}, {}
 
-        def pick(first, last, b, after=None):
+        def pick(first, last, b, after=None, between=None):
             tile = held([P, 4, (last + 1 - first) * P], F32, f"picked{first}{b}", after)
             for t in range(4):
                 nc.vector.tensor_copy(tile[:, t, :], th[4 * b + t][:].indirect(pos_sb[:, 8 * first : 8 * (last + 1)]))
+                if between is not None and t == 2:
+                    between()
             for i in range(first, last + 1):
                 picked[(i, b)] = tile[:, :, (i - first) * P : (i + 1 - first) * P]
 
@@ -215,7 +217,7 @@ def tile_list_lineage_fitness_gradients_kernel(
             for b in range(2):
                 quantise_h(i, b)
 
-        w3_w = held([P, 2 * N], I32, "w3_w", "w1_w")
+        w3_w = [held([P, N], I32, "w3_w0"), held([P, N], I32, "w3_w1", "w2_bf0")]
         y_sc = held([P, 2, M], U8, "y_sc")
         y_w = held([P, 2, M], U32, "y_w")
         y_rows = out_0.rearrange("(g p t) m -> g p t m", g=2, t=4)
@@ -229,7 +231,7 @@ def tile_list_lineage_fitness_gradients_kernel(
                     col = b * N + (4 * g + t) * P
                     nc.tensor.matmul_mx(
                         out=y_bank[(i, g)][:, t, :],
-                        lhsT=w3_w[:, col : col + P].bitcast(FP8X4),
+                        lhsT=w3_w[g][:, (4 * b + t) * P : (4 * b + t + 1) * P].bitcast(FP8X4),
                         lhsT_scale=w3_sc[W3_FIRST:P, col : col + P],
                         rhs=h_w[i][:, b * P : (b + 1) * P].bitcast(FP8X4),
                         rhs_scale=h_sc[i][:, b * P : (b + 1) * P],
@@ -255,17 +257,23 @@ def tile_list_lineage_fitness_gradients_kernel(
             if i == LAST:
                 nc.sync.dma_start(y_words[:, g : g + 1, :], y_w[:].bitcast(I32)[:, g : g + 1, :])
 
+        def round_w2(b):
+            nc.gpsimd.tensor_scalar(w2_dealt[b], w2_lines[b], -1.0, 0.0, ALU.mult, ALU.add)
+
+        def deal_w3(g):
+            dealt = w3_w[g][:].rearrange("p (a t u i) -> p a u t i", a=2, t=4, i=4)
+            lines = w3_raw[:].rearrange("p (a g u i t) -> p g a u t i", a=2, g=2, t=4, i=4)
+            for a in range(2):
+                nc.gpsimd.tensor_copy(out=dealt[:, a], in_=lines[:, g, a])
+
         nc.vector.tensor_copy(v2_w[:], tab2_w[:].indirect(offs2_sb[:]))
-        nc.vector.tensor_scalar_mul(w2_dealt[0], w2_lines[0], -1.0)
-        pick(0, LAST, 0)
-        quantise_w2(0)
-        nc.scalar.activation(w2_dealt[1], w2_lines[1], ACT.Copy, scale=-1.0)
-        nc.vector.tensor_copy(
-            out=w3_w[:].rearrange("p (g t m) -> p g m t", t=4, m=P),
-            in_=w3_raw[:].rearrange("p (g m t) -> p g m t", t=4, m=P),
-        )
+        round_w2(0)
+        pick(0, LAST, 0, between=lambda: quantise_w2(0))
+        round_w2(1)
+        deal_w3(0)
         pick(0, LAST - 1, 1)
         quantise_w2(1)
+        deal_w3(1)
         opening = ((0, 0), (1, 0), (0, 1))
         for i, b in opening + ((1, 1), (2, 0), (2, 1)):
             square(i, b)

@@ -65,7 +65,7 @@ def tile_list_lineage_fitness_gradients_kernel(
         tab_w = [held([P, T], U32, f"tab_w{a}") for a in range(2)]
         bias_sb = held([P, 2, 4], F32, "bias_sb")
         tab2_w = held([P, T2], U32, "tab2_w")
-        w2_raw = [held([P, 4, 512], F32, f"w2_raw{b}") for b in range(2)]
+        w2_raw = [held([P, 4, 256], F32, f"w2_raw{q}") for q in range(4)]
         w3_raw = held([P, 2 * N], I32, "w3_raw")
         w2_rows = w2.rearrange("(p j) r -> p j r", j=4)
 
@@ -100,7 +100,8 @@ def tile_list_lineage_fitness_gradients_kernel(
         move_rows(v_sc, 0, v_sc_rows, 0, 4)
         load_tab(1, slice(AHEAD, T))
         nc.sync.dma_start(tab2_w[:].bitcast(I32), tab2_words[0].rearrange("p n i -> p (n i)").bitcast(I32))
-        nc.sync.dma_start(w2_raw[0][:], w2_rows[:, :, 0:512])
+        for q in range(4):
+            nc.sync.dma_start(w2_raw[q][:], w2_rows[:, :, 256 * q : 256 * (q + 1)])
 
         w1_w = held([P, 2 * 2 * H], U8, "w1_w")
         v2_sc_rows = held([P, M], U8, "v2_sc_rows")
@@ -113,7 +114,6 @@ def tile_list_lineage_fitness_gradients_kernel(
             for c in range(2):
                 nc.vector.tensor_copy(v_w[a][c][:], tab_w[a][:].indirect(offs_sb[:, 32 * c : 32 * (c + 1)]))
 
-        nc.sync.dma_start(w2_raw[1][:], w2_rows[:, :, 512:1024])
         nc.sync.dma_start(
             w3_raw[:].rearrange("p (a c) -> p a c", a=2),
             w3_words.rearrange("a p n i -> a p (n i)").bitcast(I32).rearrange("a p c -> p a c"),
@@ -135,11 +135,13 @@ def tile_list_lineage_fitness_gradients_kernel(
                 stop=(a == 1),
             )
 
-        w2_w = [held([P, 512], U32, "w2_w0", "th2"), held([P, 512], U32, "w2_w1")]
+        w2_w = [held([P, 512], U32, "w2_w0", "th3"), held([P, 512], U32, "w2_w1")]
         w2_sc = [held([P, 512], U8, f"w2_sc{b}") for b in range(2)]
-        w2_bf = [held([P, 2048], BF16, f"w2_bf{b}", "w2_bf0") for b in range(2)]
-        w2_dealt = [w2_bf[b][:].rearrange("p (t m j) -> p m t j", t=4, j=4) for b in range(2)]
-        w2_lines = [w2_raw[b][:].rearrange("p j (m t) -> p m t j", t=4) for b in range(2)]
+        w2_bf = [held([P, 2048], BF16, f"w2_bf{b}") for b in range(2)]
+        w2_dealt = [
+            w2_bf[q // 2][:].rearrange("p (t u m j) -> p u m t j", t=4, u=2, j=4)[:, q % 2] for q in range(4)
+        ]
+        w2_lines = [w2_raw[q][:].rearrange("p j (m t) -> p m t j", t=4) for q in range(4)]
 
         def quantise_w2(b):
             nc.vector.quantize_mx(out=w2_w[b][:].bitcast(FP8X4), scales=w2_sc[b][:], in_=w2_bf[b][:])
@@ -161,12 +163,10 @@ def tile_list_lineage_fitness_gradients_kernel(
 
         picked, sq = {}, {}
 
-        def pick(first, last, b, after=None, between=None):
+        def pick(first, last, b, after=None):
             tile = held([P, 4, (last + 1 - first) * P], F32, f"picked{first}{b}", after)
             for t in range(4):
                 nc.vector.tensor_copy(tile[:, t, :], th[4 * b + t][:].indirect(pos_sb[:, 8 * first : 8 * (last + 1)]))
-                if between is not None and t == 2:
-                    between()
             for i in range(first, last + 1):
                 picked[(i, b)] = tile[:, :, (i - first) * P : (i + 1 - first) * P]
 
@@ -217,7 +217,8 @@ def tile_list_lineage_fitness_gradients_kernel(
             for b in range(2):
                 quantise_h(i, b)
 
-        w3_w = [held([P, N], I32, "w3_w0"), held([P, N], I32, "w3_w1", "w2_bf0")]
+        w3_codes = held([P, 2, N], I32, "w3_codes", "w2_bf0")
+        w3_w = [w3_codes[:, g] for g in range(2)]
         y_sc = held([P, 2, M], U8, "y_sc")
         y_w = held([P, 2, M], U32, "y_w")
         y_rows = out_0.rearrange("(g p t) m -> g p t m", g=2, t=4)
@@ -261,19 +262,23 @@ def tile_list_lineage_fitness_gradients_kernel(
             nc.gpsimd.tensor_scalar(w2_dealt[b], w2_lines[b], -1.0, 0.0, ALU.mult, ALU.add)
 
         def deal_w3(g):
-            dealt = w3_w[g][:].rearrange("p (a t u i) -> p a u t i", a=2, t=4, i=4)
+            dealt = w3_w[g].rearrange("p (a t u i) -> p a u t i", a=2, t=4, i=4)
             lines = w3_raw[:].rearrange("p (a g u i t) -> p g a u t i", a=2, g=2, t=4, i=4)
             for a in range(2):
                 nc.gpsimd.tensor_copy(out=dealt[:, a], in_=lines[:, g, a])
 
         nc.vector.tensor_copy(v2_w[:], tab2_w[:].indirect(offs2_sb[:]))
-        round_w2(0)
-        pick(0, LAST, 0, between=lambda: quantise_w2(0))
-        round_w2(1)
-        deal_w3(0)
+        for q in range(3):
+            round_w2(q)
+        nc.scalar.activation(
+            w2_dealt[3].rearrange("p m t j -> p m j t"), w2_lines[3].rearrange("p m t j -> p m j t"), ACT.Copy, scale=-1.0
+        )
+        pick(0, LAST, 0)
+        quantise_w2(0)
+        for g in range(2):
+            deal_w3(g)
         pick(0, LAST - 1, 1)
         quantise_w2(1)
-        deal_w3(1)
         opening = ((0, 0), (1, 0), (0, 1))
         for i, b in opening + ((1, 1), (2, 0), (2, 1)):
             square(i, b)

@@ -100,7 +100,7 @@ def tile_list_lineage_fitness_gradients_kernel(
         move_rows(v_sc, 0, v_sc_rows, 0, 4)
         load_tab(1, slice(AHEAD, T))
         nc.sync.dma_start(tab2_w[:].bitcast(I32), tab2_words[0].rearrange("p n i -> p (n i)").bitcast(I32))
-        for q in range(4):
+        for q in (0, 2, 1, 3):
             nc.sync.dma_start(w2_raw[q][:], w2_rows[:, :, 256 * q : 256 * (q + 1)])
 
         w1_w = held([P, 2 * 2 * H], U8, "w1_w")
@@ -135,7 +135,7 @@ def tile_list_lineage_fitness_gradients_kernel(
                 stop=(a == 1),
             )
 
-        w2_w = [held([P, 512], U32, "w2_w0", "th3"), held([P, 512], U32, "w2_w1")]
+        w2_w = [held([P, 512], U32, "w2_w0"), held([P, 512], U32, "w2_w1")]
         w2_sc = [held([P, 512], U8, f"w2_sc{b}") for b in range(2)]
         w2_bf = [held([P, 2048], BF16, f"w2_bf{b}") for b in range(2)]
         w2_dealt = [
@@ -268,7 +268,7 @@ def tile_list_lineage_fitness_gradients_kernel(
                 nc.gpsimd.tensor_copy(out=dealt[:, a], in_=lines[:, g, a])
 
         nc.vector.tensor_copy(v2_w[:], tab2_w[:].indirect(offs2_sb[:]))
-        for q in range(3):
+        for q in (0, 2, 1):
             round_w2(q)
         nc.scalar.activation(
             w2_dealt[3].rearrange("p m t j -> p m j t"), w2_lines[3].rearrange("p m t j -> p m j t"), ACT.Copy, scale=-1.0

@@ -217,8 +217,9 @@ def tile_list_lineage_fitness_gradients_kernel(
             for b in range(2):
                 quantise_h(i, b)
 
-        w3_codes = held([P, 2, N], I32, "w3_codes", "w2_bf0")
-        w3_w = [w3_codes[:, g] for g in range(2)]
+        w3_ahead = held([P, 3, BANK], I32, "w3_ahead", "w2_bf0")
+        w3_last = held([P, BANK], I32, "w3_last", "w2_bf1")
+        w3_w = {(0, 0): w3_ahead[:, 0], (0, 1): w3_ahead[:, 1], (1, 0): w3_ahead[:, 2], (1, 1): w3_last[:]}
         y_sc = held([P, 2, M], U8, "y_sc")
         y_w = held([P, 2, M], U32, "y_w")
         y_rows = out_0.rearrange("(g p t) m -> g p t m", g=2, t=4)
@@ -232,7 +233,7 @@ def tile_list_lineage_fitness_gradients_kernel(
                     col = b * N + (4 * g + t) * P
                     nc.tensor.matmul_mx(
                         out=y_bank[(i, g)][:, t, :],
-                        lhsT=w3_w[g][:, (4 * b + t) * P : (4 * b + t + 1) * P].bitcast(FP8X4),
+                        lhsT=w3_w[(g, b)][:, t * P : (t + 1) * P].bitcast(FP8X4),
                         lhsT_scale=w3_sc[W3_FIRST:P, col : col + P],
                         rhs=h_w[i][:, b * P : (b + 1) * P].bitcast(FP8X4),
                         rhs_scale=h_sc[i][:, b * P : (b + 1) * P],
@@ -261,11 +262,9 @@ def tile_list_lineage_fitness_gradients_kernel(
         def round_w2(b):
             nc.gpsimd.tensor_scalar(w2_dealt[b], w2_lines[b], -1.0, 0.0, ALU.mult, ALU.add)
 
-        def deal_w3(g):
-            dealt = w3_w[g].rearrange("p (a t u i) -> p a u t i", a=2, t=4, i=4)
+        def deal_w3(g, a):
             lines = w3_raw[:].rearrange("p (a g u i t) -> p g a u t i", a=2, g=2, t=4, i=4)
-            for a in range(2):
-                nc.gpsimd.tensor_copy(out=dealt[:, a], in_=lines[:, g, a])
+            nc.gpsimd.tensor_copy(out=w3_w[(g, a)].rearrange("p (t u i) -> p u t i", t=4, i=4), in_=lines[:, g, a])
 
         nc.vector.tensor_copy(v2_w[:], tab2_w[:].indirect(offs2_sb[:]))
         for q in (0, 2, 1):
@@ -275,10 +274,11 @@ def tile_list_lineage_fitness_gradients_kernel(
         )
         pick(0, LAST, 0)
         quantise_w2(0)
-        for g in range(2):
-            deal_w3(g)
+        for g, a in ((0, 0), (0, 1), (1, 0)):
+            deal_w3(g, a)
         pick(0, LAST - 1, 1)
         quantise_w2(1)
+        deal_w3(1, 1)
         opening = ((0, 0), (1, 0), (0, 1))
         for i, b in opening + ((1, 1), (2, 0), (2, 1)):
             square(i, b)

from contextlib import ExitStack

import concourse.mybir as mybir

F32 = mybir.dt.float32
BF16 = mybir.dt.bfloat16
I32 = mybir.dt.int32
U32 = mybir.dt.uint32
U16 = mybir.dt.uint16
U8 = mybir.dt.uint8
FP8X4 = mybir.dt.float8_e4m3fn_x4
FP4X4 = mybir.dt.float4_e2m1fn_x4
ACT = mybir.ActivationFunctionType
ALU = mybir.AluOpType

P = 128
K, K2, H, N, T, T2, S, M = 1024, 512, 1024, 1024, 4096, 2048, 1024, 512
BANK = 512
BANKS = 8
CHUNKS = M // P
LAST = CHUNKS - 1
V2_FIRST, W3_FIRST = 4, 8
AHEAD = T // 4
SCALAR_ROUNDS = ((LAST - 1, 0), (LAST - 1, 1), (LAST, 1))
FLOPS = 2 * (K * H * S + K2 * H * M + H * N * M)


def tile_list_lineage_fitness_gradients_kernel(
    tc, tab_words, tab_scales, offs, pos1, tab2_words, tab2_scales, offs2,
    w1_words, w1_scales, bias, w2, w3_words, w3_scales, out_0, out_1, out_2,
):
    nc = tc.nc
    with ExitStack() as ctx:
        keep = ctx.enter_context(tc.tile_pool(name="keep", bufs=1))
        acc = ctx.enter_context(tc.psum_pool(name="acc", bufs=BANKS))

        def held(shape, dtype, name, after=None):
            return keep.tile(shape, dtype, name=name, tag=after or name, align_bytes=64)

        def move_rows(plane, first, rows, start, step):
            for quad in range(0, P, 32):
                nc.sync.dma_start(
                    plane[quad + first : quad + first + 4, :].bitcast(I32),
                    rows[quad + start : quad + 32 : step, :].bitcast(I32),
                )

        def deal(dst, src, run):
            nc.vector.tensor_copy(
                out=dst.rearrange("p (g t u i) -> p g u t i", t=4, u=P // run, i=run),
                in_=src.rearrange("p (g u i t) -> p g u t i", t=4, u=P // run, i=run),
            )

        offs_sb = keep.tile([P, S // 16], U16, name="offs_sb")
        pos_sb = keep.tile([P, M // 16], U16, name="pos_sb")
        offs2_sb = keep.tile([P, M // 16], U16, name="offs2_sb")
        tab_sc = held([P, T], U8, "tab_sc")
        v_sc = held([P, 2 * S], U8, "v_sc")
        weight_sc_raw = held([P, 2 * H], U8, "weight_sc_raw")
        tab2_sc = held([P, T2], U8, "tab2_sc")
        v2_sc = held([P, M], U8, "v2_sc")
        w3_sc = held([P, 2 * N], U8, "w3_sc")
        for scale_tile in (tab_sc, tab2_sc, weight_sc_raw, v_sc, v2_sc, w3_sc):
            nc.vector.memset(scale_tile[:].bitcast(I32), 0)
        w1_raw = held([P, 2 * 2 * H], U8, "w1_raw")
        tab_w = [held([P, T], U32, f"tab_w{a}") for a in range(2)]
        bias_sb = held([P, 2, 4], F32, "bias_sb")
        tab2_w = held([P, T2], U32, "tab2_w")
        w2_raw = [held([P, 4, 256], F32, f"w2_raw{q}") for q in range(4)]
        w3_raw = held([P, 2 * N], I32, "w3_raw")
        w2_rows = w2.rearrange("(p j) r -> p j r", j=4)

        def load_tab(a, cols):
            words = tab_words[a].rearrange("p n i -> p (n i)").bitcast(I32)
            nc.sync.dma_start(tab_w[a][:].bitcast(I32)[:, cols], words[:, cols])

        nc.sync.dma_start(offs_sb[:], offs)
        nc.sync.dma_start(
            w1_raw[:].bitcast(I32).rearrange("p (a c) -> p a c", a=2),
            w1_words.bitcast(I32).rearrange("a p c -> p a c"),
        )
        nc.sync.dma_start(tab_sc[0:P:4, :].bitcast(I32), tab_scales.bitcast(I32).rearrange("a q c -> q a c"))
        nc.sync.dma_start(offs2_sb[:], offs2)
        nc.sync.dma_start(pos_sb[:], pos1)
        nc.sync.dma_start(bias_sb[:], bias.rearrange("(b p t) -> p b t", b=2, t=4))
        load_tab(0, slice(0, T // 2))
        nc.sync.dma_start(tab2_sc[4:P:8, :].bitcast(I32), tab2_scales[0].bitcast(I32))
        nc.sync.dma_start(
            weight_sc_raw[4:P:8, :].bitcast(I32).rearrange("q (a c) -> q a c", a=2),
            w3_scales.bitcast(I32).rearrange("a q c -> q a c"),
        )
        w1_scale_rows = w1_scales.bitcast(I32).rearrange("a (q r) c -> r q a c", r=4)
        for r in range(4):
            nc.sync.dma_start(
                weight_sc_raw[r:P:32, :].bitcast(I32).rearrange("q (a c) -> q a c", a=2), w1_scale_rows[r]
            )
        load_tab(0, slice(T // 2, T))
        load_tab(1, slice(0, AHEAD))
        v_sc_rows = held([P, S], U8, "v_sc_rows")
        nc.vector.tensor_copy(v_sc_rows[:], tab_sc[:].indirect(offs_sb[:]))
        move_rows(v_sc, 0, v_sc_rows, 0, 4)
        load_tab(1, slice(AHEAD, T))
        nc.sync.dma_start(tab2_w[:].bitcast(I32), tab2_words[0].rearrange("p n i -> p (n i)").bitcast(I32))
        for q in (0, 2, 1, 3):
            nc.sync.dma_start(w2_raw[q][:], w2_rows[:, :, 256 * q : 256 * (q + 1)])

        w1_w = held([P, 2 * 2 * H], U8, "w1_w")
        v2_sc_rows = held([P, M], U8, "v2_sc_rows")
        nc.vector.tensor_copy(v2_sc_rows[:], tab2_sc[:].indirect(offs2_sb[:]))
        deal(w1_w[:].bitcast(U16), w1_raw[:].bitcast(U16), 8)
        weight_sc = held([P, 2 * H], U8, "weight_sc")
        v_w = [[held([P, BANK], U32, f"v_w{a}{c}") for c in range(2)] for a in range(2)]
        deal(weight_sc[:], weight_sc_raw[:], 16)
        for a in range(2):
            for c in range(2):
                nc.vector.tensor_copy(v_w[a][c][:], tab_w[a][:].indirect(offs_sb[:, 32 * c : 32 * (c + 1)]))

        nc.sync.dma_start(
            w3_raw[:].rearrange("p (a c) -> p a c", a=2),
            w3_words.rearrange("a p n i -> a p (n i)").bitcast(I32).rearrange("a p c -> p a c"),
        )
        move_rows(v2_sc, V2_FIRST, v2_sc_rows, 4, 8)
        move_rows(w3_sc, W3_FIRST, weight_sc, 4, 8)

        th = [held([P, S], F32, f"th{s}") for s in range(8)]

        def pre_pass(bank, s, c, a):
            col = a * H + s * P
            nc.tensor.matmul_mx(
                out=bank[:],
                lhsT=w1_w[:, 2 * col : 2 * (col + P)].bitcast(FP4X4),
                lhsT_scale=weight_sc[:, col : col + P],
                rhs=v_w[a][c][:].bitcast(FP8X4),
                rhs_scale=v_sc[:, a * S + c * BANK : a * S + (c + 1) * BANK],
                start=(a == 0),
                stop=(a == 1),
            )

        w2_w = [held([P, 512], U32, "w2_w0"), held([P, 512], U32, "w2_w1")]
        w2_sc = [held([P, 512], U8, f"w2_sc{b}") for b in range(2)]
        w2_bf = [held([P, 2048], BF16, f"w2_bf{b}") for b in range(2)]
        w2_dealt = [
            w2_bf[q // 2][:].rearrange("p (t u m j) -> p u m t j", t=4, u=2, j=4)[:, q % 2] for q in range(4)
        ]
        w2_lines = [w2_raw[q][:].rearrange("p j (m t) -> p m t j", t=4) for q in range(4)]

        def quantise_w2(b):
            nc.vector.quantize_mx(out=w2_w[b][:].bitcast(FP8X4), scales=w2_sc[b][:], in_=w2_bf[b][:])

        order = [(0, 0), (1, 0), (0, 1), (1, 1)] + [(s, c) for s in range(2, 8) for c in range(2)]
        pre_bank = {}
        for s, c in sorted(order[:BANKS], key=lambda sc: sc[1]):
            pre_bank[(s, c)] = acc.tile([P, BANK], F32, name="bank")
            pre_pass(pre_bank[(s, c)], s, c, 0)
        for s, c in order:
            if (s, c) not in pre_bank:
                pre_bank[(s, c)] = acc.tile([P, BANK], F32, name="bank")
                pre_pass(pre_bank[(s, c)], s, c, 0)
            pre_pass(pre_bank[(s, c)], s, c, 1)
            nc.scalar.activation(
                th[s][:, c * BANK : (c + 1) * BANK], pre_bank[(s, c)][:], ACT.Tanh,
                bias=bias_sb[:, s // 4, s % 4 : s % 4 + 1],
            )

        picked, sq = {}, {}

        def pick(first, last, b, after=None):
            tile = held([P, 4, (last + 1 - first) * P], F32, f"picked{first}{b}", after)
            for t in range(4):
                nc.vector.tensor_copy(tile[:, t, :], th[4 * b + t][:].indirect(pos_sb[:, 8 * first : 8 * (last + 1)]))
            for i in range(first, last + 1):
                picked[(i, b)] = tile[:, :, (i - first) * P : (i + 1 - first) * P]

        v2_w = held([P, M], U32, "v2_w")
        h_bf = [held([P, 2 * BANK], BF16, f"h_bf{i}") for i in range(CHUNKS)]
        h_w = [held([P, 2 * P], U32, f"h_w{i}") for i in range(CHUNKS)]
        h_sc = [held([P, 2 * P], U8, f"h_sc{i}") for i in range(CHUNKS)]

        def square(i, b, after=None):
            sq[(i, b)] = held([P, P, 4], F32, f"sq{i}{b}", after)
            nc.scalar.activation(
                sq[(i, b)][:].rearrange("p (c i) t -> p c t i", i=4),
                picked[(i, b)].rearrange("p t (c i) -> p c t i", i=4),
                ACT.Square,
            )

        def make_h(i, b):
            cols = slice(i * P, (i + 1) * P)
            minus_err = acc.tile([P, 4, P], F32, name="bank")
            for t in range(4):
                nc.tensor.matmul_mx(
                    out=minus_err[:, t, :],
                    lhsT=w2_w[b][:, t * P : (t + 1) * P].bitcast(FP8X4),
                    lhsT_scale=w2_sc[b][:, t * P : (t + 1) * P],
                    rhs=v2_w[:, cols].bitcast(FP8X4),
                    rhs_scale=v2_sc[V2_FIRST:P, cols],
                    start=True,
                    stop=True,
                )
            nc.vector.scalar_tensor_tensor(
                out=h_bf[i][:, b * BANK : (b + 1) * BANK].rearrange("p (m t) -> p m t", t=4),
                in0=sq[(i, b)][:],
                scalar=1.0,
                in1=minus_err[:].rearrange("p t m -> p m t"),
                op0=ALU.subtract,
                op1=ALU.mult,
            )

        def quantise_h(i, b):
            cols = slice(b * P, (b + 1) * P)
            nc.vector.quantize_mx(
                out=h_w[i][:, cols].bitcast(FP8X4), scales=h_sc[i][:, cols], in_=h_bf[i][:, b * BANK : (b + 1) * BANK]
            )

        def finish_h(i):
            for b in range(2):
                make_h(i, b)
            for b in range(2):
                quantise_h(i, b)

        w3_ahead = held([P, 3, BANK], I32, "w3_ahead", "w2_bf0")
        w3_last = held([P, BANK], I32, "w3_last", "w2_bf1")
        w3_w = {(0, 0): w3_ahead[:, 0], (0, 1): w3_ahead[:, 1], (1, 0): w3_ahead[:, 2], (1, 1): w3_last[:]}
        y_sc = held([P, 2, M], U8, "y_sc")
        y_w = held([P, 2, M], U32, "y_w")
        y_rows = out_0.rearrange("(g p t) m -> g p t m", g=2, t=4)
        y_words = out_1.rearrange("g p m i -> g p (m i)").bitcast(I32).rearrange("g p m -> p g m")
        y_bank, y_sb = {}, {}

        def sum_and_store(i, g):
            y_bank[(i, g)] = acc.tile([P, 4, P], F32, name="bank")
            for b in range(2):
                for t in range(4):
                    col = b * N + (4 * g + t) * P
                    nc.tensor.matmul_mx(
                        out=y_bank[(i, g)][:, t, :],
                        lhsT=w3_w[(g, b)][:, t * P : (t + 1) * P].bitcast(FP8X4),
                        lhsT_scale=w3_sc[W3_FIRST:P, col : col + P],
                        rhs=h_w[i][:, b * P : (b + 1) * P].bitcast(FP8X4),
                        rhs_scale=h_sc[i][:, b * P : (b + 1) * P],
                        start=(b == 0 and t == 0),
                        stop=(b == 1 and t == 3),
                    )
            y_sb[(i, g)] = held([P, 4, P], F32, f"y_sb{i}{g}")
            nc.scalar.copy(y_sb[(i, g)][:], y_bank[(i, g)][:])
            nc.sync.dma_start(y_rows[g][:, :, i * P : (i + 1) * P], y_sb[(i, g)][:])

        def quantise_y(i, g, woven):
            if (i, g) in SCALAR_ROUNDS:
                nc.scalar.copy(woven, y_bank[(i, g)][:].rearrange("p t m -> p m t"))
            else:
                nc.vector.tensor_copy(
                    woven.rearrange("p (c i) t -> p c t i", i=4),
                    y_sb[(i, g)][:].rearrange("p t (c i) -> p c t i", i=4),
                )
            cols = slice(i * P, (i + 1) * P)
            nc.vector.quantize_mx(
                out=y_w[:, g, cols].bitcast(FP8X4), scales=y_sc[:, g, cols], in_=woven.rearrange("p m t -> p (m t)")
            )
            if i == LAST:
                nc.sync.dma_start(y_words[:, g : g + 1, :], y_w[:].bitcast(I32)[:, g : g + 1, :])

        def round_w2(b):
            nc.gpsimd.tensor_scalar(w2_dealt[b], w2_lines[b], -1.0, 0.0, ALU.mult, ALU.add)

        def deal_w3(g, a):
            lines = w3_raw[:].rearrange("p (a g u i t) -> p g a u t i", a=2, g=2, t=4, i=4)
            nc.gpsimd.tensor_copy(out=w3_w[(g, a)].rearrange("p (t u i) -> p u t i", t=4, i=4), in_=lines[:, g, a])

        nc.vector.tensor_copy(v2_w[:], tab2_w[:].indirect(offs2_sb[:]))
        for q in (0, 2, 1):
            round_w2(q)
        nc.scalar.activation(
            w2_dealt[3].rearrange("p m t j -> p m j t"), w2_lines[3].rearrange("p m t j -> p m j t"), ACT.Copy, scale=-1.0
        )
        pick(0, LAST, 0)
        quantise_w2(0)
        for g, a in ((0, 0), (0, 1), (1, 0)):
            deal_w3(g, a)
        pick(0, LAST - 1, 1)
        quantise_w2(1)
        deal_w3(1, 1)
        opening = ((0, 0), (1, 0), (0, 1))
        for i, b in opening + ((1, 1), (2, 0), (2, 1)):
            square(i, b)
        for i, b in opening:
            make_h(i, b)
        for i, b in opening:
            quantise_h(i, b)
        make_h(1, 1)
        pick(LAST, LAST, 1, "sq01")
        quantise_h(1, 1)
        finish_h(2)
        sum_and_store(0, 0)
        square(LAST, 0)
        sum_and_store(0, 1)
        for g in range(2):
            sum_and_store(1, g)
        square(LAST, 1, "h_bf1")
        finish_h(LAST)
        for i in (LAST - 1, LAST):
            for g in range(2):
                sum_and_store(i, g)
        y_bf = held([P, 2 * CHUNKS, P, 4], BF16, "y_bf", "sq01")
        for i in range(CHUNKS):
            for g in range(2):
                quantise_y(i, g, y_bf[:, 2 * i + g])
        y_scale_rows = out_2.bitcast(I32).rearrange("g q m -> q g m")
        for quad in range(4):
            nc.scalar.dma_start(
                y_scale_rows[4 * quad : 4 * quad + 4], y_sc[32 * quad : 32 * quad + 4].bitcast(I32)
            )
